import numpy as np, ml_dtypes
CORES = [8,9,10,11,12,13]
N = 6
import mx_ref
BF = ml_dtypes.bfloat16
def entries(a):
    return np.ascontiguousarray(a.T).reshape(-1)
def table(e):
    return np.ascontiguousarray(np.reshape(e, (-1, 16)).T).astype(np.int32)
def cols(t, e):
    v = np.concatenate([t.reshape(128, -1, 4), np.zeros((128, 1, 4), BF)], axis=1)
    return np.ascontiguousarray(v[:, e]).reshape(128, -1)
def cut(t, i, w=512):
    return t[:, w * i:w * i + w]
def f(rng, *shape):
    return mx_ref.flush((rng.standard_normal(shape, dtype=np.float32) * np.exp2(rng.integers(-2, 3, shape[:-1] + (1,)))).astype(BF))
def wide(rng, *shape, cols=0):
    v = rng.standard_normal(shape, dtype=np.float32) * np.exp2(rng.integers(-12, 13, shape)).astype(np.float32)
    if cols: v *= np.repeat(np.exp2(rng.integers(-cols, cols + 1, shape[:-2] + (1, shape[-1] // 4))) * (rng.random(shape[:-2] + (1, shape[-1] // 4)) > 0.0625), 4, axis=-1).astype(np.float32)
    return mx_ref.flush(v.astype(BF))
T, O = 256, 2
def places(rng, dest):
    e = np.zeros((N, T), int)
    for d in range(N): e[dest == d] = d * T + rng.permutation(T)
    return np.stack([table(e[r]) for r in range(N)])
def relabel(rng):
    p = rng.permutation(N)
    if np.all((p - np.arange(N)) % N == p[0]): p[[0, 1]] = p[[1, 0]]
    return p
def setup_inputs(rng):
    e = rng.permutation(N * T).reshape(N, T)
    return {"x": f(rng, N, 128, 4 * T), "to": np.stack([table(e[r]) for r in range(N)]), "w": f(rng, N, 128, 512 * O)}
def setup_inputs_swap(rng):
    d = setup_inputs(rng); p = rng.permutation(N); dest = np.zeros((N, T), int)
    for k in range(N): dest[p[k]] = p[(k + 1) % N]
    d["to"] = places(rng, dest); return d
def setup_inputs_ones(rng):
    d = setup_inputs(rng); i = np.arange(N); n = np.ones((N, N), int); n[i, rng.permutation(N)] += T % N
    for t in range(T // N - 1): n[i, rng.permutation(N)] += N
    d["to"] = places(rng, np.stack([rng.permutation(np.repeat(i, n[r])) for r in range(N)])); return d
def setup_inputs_runs(rng):
    d = setup_inputs(rng); p = relabel(rng); s, u = rng.integers(1, N), rng.integers(0, N); g, h = rng.permutation(N), rng.permutation(N)
    n = T // N + ((g[:, None] + h) % N < T % N)
    j = (np.arange(N) + s * np.arange(N)[:, None] + u) % N
    d["to"] = places(rng, np.stack([np.repeat(p[j[r]], n[r, j[r]]) for r in range(N)])); return d
def setup_inputs_comb(rng):
    d = setup_inputs(rng); p = relabel(rng); s, u = rng.integers(1, N), rng.integers(0, N); k = rng.permutation(N); c = np.arange(T)
    d["to"] = places(rng, np.stack([p[(c + np.where(c < T - T % N, s * r + u, k[r])) % N] for r in range(N)])); return d
def setup_inputs_spread(rng):
    d = setup_inputs(rng); d["x"] = wide(rng, N, 128, 4 * T, cols=8); return d
def check_inputs(d):
    e = np.concatenate([entries(d["to"][r]) for r in range(N)])
    return [] if np.array_equal(np.sort(e), np.arange(N * T)) else ["to"]
def reference(x, to, w):
    z = np.concatenate([x[r] for r in range(N)], axis=1)
    e = np.concatenate([entries(to[r]) for r in range(N)])
    home = np.zeros(N * T, int); home[e] = np.arange(N * T)
    y = np.zeros((N, 128, O * T), np.float32)
    for d in range(N):
        v = mx_ref.quantize(cols(z, home[d * T:d * T + T]))
        for o in range(O): y[d][:, T * o:T * o + T] = mx_ref.matmul(mx_ref.quantize(np.ascontiguousarray(cut(w[d], o))), v)
    return {"y": y}

@@ -1,0 +1,394 @@
+from concourse.bass import DstId, RemoteDMATransfer
+from concourse.mybir import dt, AluOpType, ActivationFunctionType
+
+N = 6
+C1, C2 = 43, 48
+OWN = 48
+W1 = OWN + 5 * C1
+
+
+def _sb(n, d, rows=128):
+    return ("sbuf", [rows, n], d)
+
+
+_C = "float8_e4m3fn_x4"
+SCRATCH = {
+    "toh": _sb(8, "int32"), "xs": _sb(1024, "bfloat16"), "ws": _sb(1024, "bfloat16"),
+    "p8": _sb(16, "int32"), "Dc": _sb(48, "int32"), "kk": _sb(10, "int32"), "dupb": _sb(4, "int32"),
+    "R8r": _sb(144, "float32"), "R8": _sb(144, "float32"), "cvr": _sb(128, "float32"), "cval": _sb(128, "bfloat16"),
+    "idt": _sb(256, "bfloat16"), "Jr": _sb(144, "float32"), "J": _sb(144, "float32"), "J2r": _sb(18, "float32"),
+    "J2": _sb(18, "float32"), "c6": _sb(8, "float32"), "c6b": _sb(8, "float32"),
+    "p7i": _sb(8, "int32"), "b3": _sb(10, "int32"), "qi": _sb(4, "int32"), "h1": _sb(1, "int32"),
+    "repa": _sb(8, "uint16"), "repdi": _sb(10, "int32"), "repd": _sb(10, "uint16"), "dupi": _sb(4, "int32"),
+    "dup": _sb(4, "uint16"), "hf": _sb(1, "float32"), "qf": _sb(1, "float32"), "p7f": _sb(1, "float32"),
+    "p78f": _sb(1, "float32"), "lg": _sb(6, "uint16"), "tt3": _sb(10, "int32"), "rl": _sb(10, "uint16"),
+    "cb": _sb(48, "float32"), "zer": _sb(32, "float32"),
+    "dest": _sb(8, "int32"), "tou": _sb(8, "uint16"), "H": _sb(48, "float32"), "Cb": _sb(256, "float32"),
+    "Tr": _sb(32, "float32"), "QQ": _sb(64, "float32"), "Z": _sb(64, "float32"), "Sb": _sb(8, "bfloat16"),
+    "K": _sb(8, "float32"), "Xk": _sb(48, "float32"), "Xm": _sb(48, "float32"), "a1": _sb(24, "float32"),
+    "a2": _sb(8, "float32"), "P": _sb(8, "float32"), "Pu": _sb(8, "uint16"), "P6": _sb(8, "int32"),
+    "P48": _sb(8, "float32"), "T1": _sb(8, "float32"), "e1": _sb(8, "float32"), "off1": _sb(8, "uint16"),
+    "win1": _sb(288, "bfloat16"), "tr1": _sb(288, "bfloat16"),
+    "Y1": _sb(32, "float32"), "Yt1": _sb(32, "float32"), "Yd1": _sb(64, "float32"), "Z1": _sb(64, "float32"),
+    "l1": _sb(18, "uint16"), "l1o": _sb(4, "uint16"),
+    "Pf": _sb(128, "bfloat16"), "keywin": _sb(1536, "bfloat16"), "trk": _sb(1536, "bfloat16"),
+    "Xs": _sb(48, "bfloat16"), "Xin": _sb(48, "bfloat16"),
+    "cnt": _sb(64, "bfloat16"), "G": _sb(96, "float32"), "Nn": _sb(48, "float32"), "Lf": _sb(48, "int32"),
+    "Ai": _sb(48, "float32"), "off": _sb(48, "float32"), "FF": _sb(56, "int32"), "Bt": _sb(48, "float32"),
+    "U": _sb(48, "float32"), "Vv": _sb(48, "float32"), "DD": _sb(48, "float32"), "off2": _sb(8, "float32"),
+    "GE": _sb(144, "float32"), "M": _sb(144, "float32"), "Sm": _sb(144, "float32"), "lf": _sb(18, "float32"),
+    "l2": _sb(18, "uint16"), "l2o": _sb(4, "uint16"),
+    "P6x": _sb(48, "int32"), "tx": _sb(48, "float32"), "u6": _sb(48, "int32"), "mk": _sb(48, "float32"),
+    "V1": _sb(48, "float32"), "V2": _sb(48, "float32"), "V3": _sb(48, "float32"), "V4": _sb(48, "float32"),
+    "Wx": _sb(48, "float32"), "b1": _sb(24, "float32"), "b2": _sb(8, "float32"),
+    "Y2": _sb(32, "float32"), "Yt2": _sb(32, "float32"), "Yd2": _sb(64, "float32"), "Z2": _sb(64, "float32"),
+    "l3": _sb(16, "uint16"),
+    "qx": _sb(256, _C), "sx": _sb(256, "uint8"), "qw": _sb(256, _C), "sw": _sb(256, "uint8"),
+    "q1": _sb(288, _C), "s1": _sb(288, "uint8"), "land1": _sb(W1 + 1, _C), "lans1": _sb(W1 + 1, "uint8"),
+    "q2": _sb(288, _C), "s2": _sb(288, "uint8"), "land2": _sb(288, _C), "lans2": _sb(288, "uint8"),
+    "q3": _sb(256, _C), "s3": _sb(256, "uint8"),
+    "ps": ("psum", [128, 2048], "float32"), "ys": _sb(512, "float32"),
+}
+SEMAPHORES = ["v", "gi1", "gi2", "to_in", "x_in", "w_in", "sb", "p_ok", "pf", "kz", "l1r", "l1own", "qxr", "q1c", "q1s",
+              "o1c", "o1s", "xsr", "xown", "cown", "l2r", "l2own", "q2c", "q2s", "o2c", "o2s", "l3r", "qwr",
+              "q3c0", "q3c1", "q3s0", "q3s1", "mm00", "mm01", "mm10", "mm11", "y0", "y1", "st",
+              "rc", "rx", "rc1", "rs1", "rc2", "rs2", "ls"]
+
+
+def _shares(src, cores, topo, flip):
+    ds = [c for c in cores if c != src]
+    k = ds.index([c for c in cores + cores if c != src and cores.index(c) > cores.index(src)][0]) if src != cores[-1] else 0
+    ds = ds[k:] + ds[:k]
+    ds = sorted(ds, key=lambda c: topo.die(c) == topo.die(src))
+    e = topo.engines(src, ds[0])
+    w = len(e) // 4
+    if flip:
+        e = e[w:] + e[:w]
+    out = {}
+    for i, c in enumerate(ds):
+        if i < 3:
+            out[c] = e[i * w:(i + 1) * w]
+        else:
+            h = w // 2
+            out[c] = e[3 * w + (i - 3) * h:3 * w + (i - 2) * h]
+    return out
+
+
+def rank_program(g, core, T, topo):
+    R = T.rank_of(core)
+    if R is None:
+        return
+    cores = list(T.cores)
+    V, A, S, E = g.vector, g.scalar, g.sync, g.tensor
+    add, sub, mul = AluOpType.add, AluOpType.subtract, AluOpType.mult
+    mn, mx = AluOpType.min, AluOpType.max
+    eq, gt, le = AluOpType.is_equal, AluOpType.is_gt, AluOpType.is_le
+    shr, band = AluOpType.arith_shift_right, AluOpType.bitwise_and
+    Copy = ActivationFunctionType.Copy
+    tot = {}
+
+    def inc(inst, sem, n=1):
+        inst.then_inc(T.sem[sem], n)
+        tot[sem] = tot.get(sem, 0) + n
+
+    waited = [0]
+
+    def v(inst, sem="v"):
+        inc(inst, sem)
+
+    def vw():
+        if tot.get("v", 0) > waited[0]:
+            V.wait_ge(T.sem.v, tot["v"])
+            waited[0] = tot["v"]
+
+    def w(q, sem, n):
+        q.wait_ge(T.sem[sem], n)
+
+    def base1(r, m):
+        return 0 if r == m else OWN + C1 * [k for k in range(N) if k != m].index(r)
+
+    def arrivals(flip):
+        return sum(len(_shares(c, cores, topo, flip)[core]) for c in cores if c != core)
+
+    def fused(src_of, dst_of, sem, flip):
+        sh = _shares(core, cores, topo, flip)
+        tr = []
+        for c in sh:
+            rid, pid, _ = topo.addr(c)
+            d = cores.index(c)
+            tr.append(RemoteDMATransfer(dst_ids=[DstId(rid=rid, pnc=pid)], dma_engine_mask=sum(1 << e for e in sh[c]),
+                                        remote_sem=T.sem[sem], src=src_of(d), dst=dst_of(d)))
+            tot["ls"] = tot.get("ls", 0) + len(sh[c])
+        g.remote_dma_fused(tr, local_sem=T.sem.ls)
+
+    for b in range(4):
+        for h in range(2):
+            q = S if h == 0 else A
+            inc(q.dma_start(T.toh[32 * b + 16 * h:32 * b + 16 * h + 16, :], T.to[:, 8 * h:8 * h + 8]), "to_in", 16)
+    inc(S.dma_start(T.xs[:, 0:512], T.x[:, 0:512]), "x_in", 16)
+    inc(A.dma_start(T.xs[:, 512:1024], T.x[:, 512:1024]), "x_in", 16)
+    inc(S.dma_start(T.ws[:, 0:1024], T.w[:, 0:1024]), "w_in", 16)
+
+    inc(g.iota(T.p8[:], [[0, 16]], 0, 1), "gi1")
+    inc(g.iota(T.kk[:], [[2, 10]], 0, 0), "gi1")
+    inc(g.iota(T.dupb[:], [[16, 2], [0, 2]], 0, 0), "gi1")
+    inc(g.iota(T.Dc[:], [[1, 6], [0, 8]], 0, 0), "gi1")
+    inc(g.iota(T.R8r[:], [[0, 18], [1, 8]], 0, 0, allow_small_or_imprecise_dtypes=True), "gi1")
+    inc(g.iota(T.cvr[:], [[1, 128]], 0, 0, allow_small_or_imprecise_dtypes=True), "gi1")
+    inc(g.iota(T.idt[:], [[1, 256]], 1, 0, allow_small_or_imprecise_dtypes=True), "gi2")
+    inc(g.iota(T.c6[:], [[6, 8]], 0, 0, allow_small_or_imprecise_dtypes=True), "gi2")
+    inc(g.iota(T.J2r[:], [[0, 6], [16, 3]], 0, 0, allow_small_or_imprecise_dtypes=True), "gi2")
+    inc(g.iota(T.Jr[:], [[0, 6], [16, 3], [-1, 8]], 0, 0, allow_small_or_imprecise_dtypes=True), "gi2")
+
+    v(V.memset(T.zer[:], 0.0))
+    v(V.memset(T.Cb[:, 48:256], 0.0))
+    v(V.memset(T.Sb[:], 0.0))
+    v(V.memset(T.Y1[:], 0.0))
+    v(V.memset(T.Y2[:], 0.0))
+    v(V.memset(T.win1[:], 0.0))
+    v(V.memset(T.cnt[:, 48:64], 0.0))
+    v(V.memset(T.FF[:], 0))
+    v(V.memset(T.cb[:], 0.0))
+    w(V, "gi1", tot["gi1"])
+    v(V.tensor_scalar(T.p7i[:], T.p8[:, 0:8], 7, None, band))
+    v(V.tensor_scalar(T.b3[:], T.p8[:, 0:10], 3, 1, shr, band))
+    v(V.tensor_scalar(T.qi[:], T.p8[:, 0:4], 15, None, band))
+    v(V.tensor_scalar(T.h1[:], T.p8[:, 0:1], 4, 1, shr, band))
+    v(V.tensor_scalar(T.R8[:], T.R8r[:], 1.0, None, mn))
+    vw()
+    v(V.tensor_copy(T.repa[:], T.p7i[:]))
+    v(V.tensor_tensor(T.repdi[:], T.b3[:], T.kk[:], add))
+    v(V.tensor_tensor(T.dupi[:], T.qi[:], T.dupb[:], add))
+    v(V.tensor_scalar(T.hf[:], T.h1[:], 128.0, None, mul))
+    v(V.tensor_copy(T.qf[:], T.qi[:, 0:1]))
+    v(V.tensor_copy(T.p7f[:], T.p7i[:, 0:1]))
+    v(V.tensor_scalar(T.p78f[:], T.p7i[:, 0:1], 8.0, None, mul))
+    for r in range(N):
+        d = base1(r, R) - r - (base1(r - 1, R) - (r - 1) if r else 0)
+        v(V.memset(T.cb[:, r:48:8], float(d)))
+    vw()
+    v(V.tensor_copy(T.repd[:], T.repdi[:]))
+    v(V.tensor_copy(T.dup[:], T.dupi[:]))
+    v(V.tensor_scalar(T.cval[:], T.cvr[:], T.hf[:, 0:1], None, add))
+
+    w(V, "to_in", tot["to_in"])
+    v(V.tensor_scalar(T.dest[:], T.toh[:], 8, None, shr))
+    vw()
+    v(V.tensor_tensor(T.H[:], T.dest[:, 0:8].indirect(T.repa[:, 0:3]), T.Dc[:], eq))
+    vw()
+    v(V.tensor_tensor_scan(T.Cb[:, 0:48], T.R8[:, 0:48], T.H[:], 0.0, mul, add))
+    vw()
+    v(V.transpose(T.Tr[:], T.Cb[:, 7:256:8]))
+    vw()
+    v(V.tensor_tensor_scan(T.QQ[:, 0:32], T.Tr[:], T.zer[:], 0.0, add, add))
+    vw()
+    v(V.tensor_scalar(T.QQ[:, 32:64], T.zer[:], T.QQ[:, 31:32], None, add))
+    vw()
+    v(V.transpose(T.Z[:], T.QQ[:]))
+    vw()
+    v(V.tensor_tensor_scan(T.Sb[:, 1:7], T.Z[:, 32:38], T.zer[:, 0:6], 0.0, add, add), "sb")
+    w(V, "sb", 1)
+    v(V.tensor_tensor(T.K[:, 0:6], T.Z[:, 0:6], T.Sb[:, 0:6], add))
+    vw()
+    v(V.tensor_tensor(T.Xk[:], T.K[:, 0:6].indirect(T.repd[:, 0:3]), T.Cb[:, 0:48], sub))
+    vw()
+    v(V.tensor_tensor(T.Xm[:], T.Xk[:], T.H[:], mul))
+    vw()
+    v(V.tensor_tensor(T.a1[:], T.Xm[:, 0:24], T.Xm[:, 24:48], add))
+    vw()
+    v(V.tensor_tensor(T.a2[:], T.a1[:, 0:8], T.a1[:, 8:16], add))
+    vw()
+    v(V.tensor_tensor(T.P[:], T.a2[:], T.a1[:, 16:24], add))
+    vw()
+    v(V.tensor_scalar(T.P6[:], T.P[:], 1.0 / 6, -2.5 / 6, mul, add))
+    v(V.tensor_scalar(T.P48[:], T.P[:], 48.0, None, mul))
+    v(V.tensor_copy(T.Pu[:], T.P[:]), "p_ok")
+    vw()
+    v(V.tensor_scalar(T.T1[:], T.P6[:], -287.0, None, mul))
+    vw()
+    v(V.tensor_tensor(T.e1[:], T.T1[:], T.P48[:], add))
+    vw()
+    v(V.tensor_copy(T.off1[:], T.e1[:]))
+    w(V, "x_in", tot["x_in"])
+    v(V.quantize_mx(T.qx[:], T.sx[:], T.xs[:]), "qxr")
+    vw()
+    v(V.tensor_copy(T.win1[:, 0:288].indirect(T.off1[:, 0:8]), T.cval[:]))
+    vw()
+    v(V.transpose(T.tr1[:], T.win1[:]))
+    vw()
+
+    def across(Y, Yt, Yd, Zz, lst, nb, sem):
+        v(V.transpose(Yt[:], Y[:]))
+        vw()
+        v(V.tensor_copy(Yd[:], Yt[:].indirect(T.dup[:, 0:4])))
+        vw()
+        v(V.transpose(Zz[:], Yd[:]))
+        vw()
+        v(V.tensor_copy(lst[:, 0:2 * nb:2], Zz[:, 0:nb]), sem)
+        v(V.tensor_copy(lst[:, 1:2 * nb:2], Zz[:, 32:32 + nb]), sem)
+        w(V, sem, 2)
+
+    v(V.tensor_tensor(T.Y1[:, 0:9], T.tr1[:, 0:288:32], T.tr1[:, 16:288:32], add))
+    vw()
+    across(T.Y1, T.Yt1, T.Yd1, T.Z1, T.l1, 9, "l1r")
+    w(V, "qxr", 1)
+
+    def pickc(out, a, b, src, n, lst, c, e):
+        return V.tensor_copy(out[:, a:b].bitcast(dt.uint32), src[:, 0:n].bitcast(dt.uint32).indirect(lst[:, c:e]))
+
+    def picks(out, a, b, src, n, lst, c, e):
+        return A.activation(out[:, a:b], src[:, 0:n].indirect(lst[:, c:e]), Copy)
+
+    v(pickc(T.q1, 0, 288, T.qx, 256, T.l1, 0, 18), "q1c")
+    v(V.tensor_copy(T.l1o[:, 0:3], T.l1[:, 3 * R:3 * R + 3]), "l1own")
+    w(V, "l1own", 1)
+    v(pickc(T.land1, 0, 48, T.qx, 256, T.l1o, 0, 3), "o1c")
+
+    w(V, "pf", 1)
+    w(V, "kz", 2)
+    v(V.tensor_copy(T.tou[:], T.toh[:]))
+    vw()
+    v(V.tensor_copy(T.keywin[:].indirect(T.tou[:, 0:8]), T.Pf[:]))
+    vw()
+    v(V.transpose(T.trk[:], T.keywin[:]))
+    vw()
+    v(V.tensor_tensor(T.Xs[:], T.trk[:, 0:1536:32], T.trk[:, 16:1536:32], add), "xsr")
+
+    w(V, "gi2", tot["gi2"])
+    v(V.tensor_scalar(T.lg[:, 0:3], T.repdi[:, 0:3], T.p78f[:, 0:1], None, add))
+    v(V.tensor_scalar(T.lg[:, 3:6], T.repdi[:, 0:3], T.p78f[:, 0:1], 1.0, add, add))
+    v(V.tensor_scalar(T.tt3[:], T.repdi[:], 1.0 / 3, -1.0 / 3, mul, add))
+    v(V.tensor_scalar(T.J[:], T.Jr[:], T.qf[:, 0:1], None, add))
+    v(V.tensor_scalar(T.J2[:], T.J2r[:], T.qf[:, 0:1], None, add))
+    v(V.tensor_scalar(T.c6b[:], T.c6[:], -291.5, None, add))
+    vw()
+    v(V.tensor_scalar(T.rl[:], T.tt3[:], 8.0, T.p7f[:, 0:1], mul, add))
+    nr = arrivals(False)
+    w(V, "rc", nr)
+    w(V, "cown", 1)
+    v(V.tensor_copy(T.G[:], T.cnt[:, 0:64].indirect(T.lg[:, 0:6])))
+    vw()
+    v(V.tensor_tensor(T.Nn[:], T.G[:, 48:96], T.G[:, 0:48], sub))
+    v(V.tensor_scalar(T.Lf[:], T.G[:, 0:48], 1.0 / 6, (5 - R) / 6 - 2.5 / 6, mul, add))
+    vw()
+    v(V.tensor_tensor_scan(T.Ai[:], T.R8[:, 0:48], T.Nn[:], 0.0, mul, add))
+    vw()
+    v(V.tensor_tensor(T.off[:], T.Ai[:], T.G[:, 48:96], sub))
+    vw()
+    v(V.tensor_scalar(T.FF[:, 1:49], T.off[:], 1.0 / 6, R / 6 - 2.5 / 6, mul, add))
+    v(V.tensor_tensor(T.off2[:, 0:6], T.off[:, 8 * R:8 * R + 6], T.c6b[:, 0:6], add))
+    vw()
+    v(V.tensor_tensor(T.Bt[:], T.Lf[:], T.FF[:, 1:49], add))
+    v(V.tensor_tensor(T.U[:], T.FF[:, 0:48], T.R8[:, 0:48], mul))
+    v(V.tensor_tensor(T.Vv[:], T.cb[:], T.FF[:, 1:49], sub))
+    vw()
+    v(V.tensor_tensor(T.GE[:], T.Bt[:].indirect(T.rl[:, 0:9]), T.J[:], le))
+    v(V.tensor_tensor(T.DD[:], T.U[:], T.Vv[:], add))
+    vw()
+    v(V.tensor_tensor(T.M[:], T.DD[:].indirect(T.rl[:, 0:9]), T.GE[:], mul))
+    vw()
+    v(V.tensor_tensor_scan(T.Sm[:], T.R8[:], T.M[:], 0.0, mul, add))
+    vw()
+    v(V.tensor_tensor(T.lf[:], T.Sm[:, 5:144:8], T.J2[:], add))
+    vw()
+    v(V.tensor_scalar(T.l2[:], T.lf[:], 0.0, float(W1 - 1), mx, mn), "l2r")
+    v(V.tensor_scalar(T.l2o[:, 0:3], T.lf[:, 3 * R:3 * R + 3], 0.0, float(W1 - 1), mx, mn), "l2own")
+    w(V, "l2r", 1)
+    w(V, "o1c", 1)
+    w(V, "rc1", arrivals(False))
+    v(pickc(T.q2, 0, 288, T.land1, W1, T.l2, 0, 18), "q2c")
+    w(V, "l2own", 1)
+    v(pickc(T.land2, 48 * R, 48 * R + 48, T.land1, W1, T.l2o, 0, 3), "o2c")
+    w(V, "w_in", tot["w_in"])
+    v(V.quantize_mx(T.qw[:], T.sw[:], T.ws[:]), "qwr")
+
+    w(V, "rx", nr)
+    w(V, "xown", 1)
+    v(V.tensor_scalar(T.P6x[:], T.Xin[:], 1.0 / 6, -3.5 / 6, mul, add))
+    v(V.tensor_tensor(T.tx[:], T.off2[:, 0:6].indirect(T.repd[:, 0:3]), T.Xin[:], add))
+    v(V.tensor_scalar(T.mk[:], T.Xin[:], 0.0, None, gt))
+    v(V.tensor_scalar(T.Wx[:], T.Xin[:], 48.0, None, mul))
+    vw()
+    v(V.tensor_scalar(T.V1[:], T.P6x[:], -288.0, None, mul))
+    v(V.tensor_scalar(T.u6[:], T.tx[:], 1.0 / 6, None, mul))
+    vw()
+    v(V.tensor_tensor(T.V2[:], T.V1[:], T.Wx[:], add))
+    vw()
+    v(V.tensor_tensor(T.V3[:], T.V2[:], T.u6[:], add))
+    vw()
+    v(V.tensor_tensor(T.V4[:], T.V3[:], T.mk[:], mul))
+    vw()
+    v(V.tensor_tensor(T.b1[:], T.V4[:, 0:24], T.V4[:, 24:48], add))
+    vw()
+    v(V.tensor_tensor(T.b2[:], T.b1[:, 0:8], T.b1[:, 8:16], add))
+    vw()
+    v(V.tensor_tensor(T.Y2[:, 0:8], T.b2[:], T.b1[:, 16:24], add))
+    vw()
+    across(T.Y2, T.Yt2, T.Yd2, T.Z2, T.l3, 8, "l3r")
+    w(V, "o2c", 1)
+    w(V, "rc2", arrivals(False))
+    for h in range(2):
+        v(pickc(T.q3, 128 * h, 128 * h + 128, T.land2, 288, T.l3, 8 * h, 8 * h + 8), "q3c%d" % h)
+    for h in range(2):
+        w(V, "mm0%d" % h, 1)
+        v(V.tensor_copy(T.ys[:, 128 * h:128 * h + 128], T.ps[:, 512 * h:512 * h + 128]), "y0")
+
+    w(E, "qwr", 1)
+    for h in range(2):
+        w(E, "q3c%d" % h, 1)
+        w(E, "q3s%d" % h, 1)
+        for o in range(2):
+            b = 512 * (2 * o + h)
+            inc(E.matmul_mx(T.ps[:, b:b + 128], T.qw[:, 128 * o:128 * o + 128], T.sw[:, 128 * o:128 * o + 128],
+                            T.q3[:, 128 * h:128 * h + 128], T.s3[:, 128 * h:128 * h + 128], True, True), "mm%d%d" % (o, h))
+
+    w(A, "x_in", tot["x_in"])
+    inc(A.activation(T.keywin[:, 0:1024], T.xs[:, 0:1024], Copy, scale=0.0), "kz")
+    inc(A.activation(T.keywin[:, 1024:1536], T.xs[:, 0:512], Copy, scale=0.0), "kz")
+    w(A, "sb", 1)
+    inc(A.activation(T.cnt[:, 8 * R:8 * R + 8], T.Sb[:], Copy), "cown")
+    w(A, "p_ok", 1)
+    w(A, "gi2", tot["gi2"])
+    inc(A.activation(T.Pf[:], T.idt[:, 0:256].indirect(T.Pu[:, 0:8]), Copy), "pf")
+    w(A, "qxr", 1)
+    w(A, "l1r", 2)
+    inc(picks(T.s1, 0, 288, T.sx, 256, T.l1, 0, 18), "q1s")
+    w(A, "l1own", 1)
+    inc(picks(T.lans1, 0, 48, T.sx, 256, T.l1o, 0, 3), "o1s")
+    w(A, "xsr", 1)
+    inc(A.activation(T.Xin[:, 8 * R:8 * R + 8], T.Xs[:, 8 * R:8 * R + 8], Copy), "xown")
+    w(A, "l2r", 1)
+    w(A, "o1s", 1)
+    w(A, "rs1", arrivals(True))
+    inc(picks(T.s2, 0, 288, T.lans1, W1, T.l2, 0, 18), "q2s")
+    w(A, "l2own", 1)
+    inc(picks(T.lans2, 48 * R, 48 * R + 48, T.lans1, W1, T.l2o, 0, 3), "o2s")
+    w(A, "l3r", 2)
+    w(A, "o2s", 1)
+    w(A, "rs2", arrivals(True))
+    for h in range(2):
+        inc(picks(T.s3, 128 * h, 128 * h + 128, T.lans2, 288, T.l3, 8 * h, 8 * h + 8), "q3s%d" % h)
+    for h in range(2):
+        w(A, "mm1%d" % h, 1)
+        inc(A.activation(T.ys[:, 256 + 128 * h:384 + 128 * h], T.ps[:, 1024 + 512 * h:1152 + 512 * h], Copy), "y1")
+    w(A, "y1", 2)
+    inc(A.dma_start(T.y[:, 256:512], T.ys[:, 256:512]), "st", 16)
+    w(S, "y0", 2)
+    inc(S.dma_start(T.y[:, 0:256], T.ys[:, 0:256]), "st", 16)
+
+    w(g, "sb", 1)
+    fused(lambda d: T.Sb[:, 0:8], lambda d: T.cnt[:, 8 * R:8 * R + 8], "rc", False)
+    w(g, "q1c", 1)
+    fused(lambda d: T.q1[:, 48 * d:48 * d + C1].bitcast(dt.uint8),
+          lambda d: T.land1[:, base1(R, d):base1(R, d) + C1].bitcast(dt.uint8), "rc1", False)
+    w(g, "q1s", 1)
+    fused(lambda d: T.s1[:, 48 * d:48 * d + C1], lambda d: T.lans1[:, base1(R, d):base1(R, d) + C1], "rs1", True)
+    w(g, "xsr", 1)
+    fused(lambda d: T.Xs[:, 8 * d:8 * d + 8], lambda d: T.Xin[:, 8 * R:8 * R + 8], "rx", False)
+    w(g, "q2c", 1)
+    fused(lambda d: T.q2[:, 48 * d:48 * d + C2].bitcast(dt.uint8),
+          lambda d: T.land2[:, 48 * R:48 * R + C2].bitcast(dt.uint8), "rc2", False)
+    w(g, "q2s", 1)
+    fused(lambda d: T.s2[:, 48 * d:48 * d + C2], lambda d: T.lans2[:, 48 * R:48 * R + C2], "rs2", True)
+    for s in ("v", "ls", "st"):
+        w(g, s, tot[s])

@@ -5,73 +5,38 @@ N = 6
 C1, C2 = 43, 48
 OWN = 48
 W1 = OWN + 5 * C1
-
-
-def _sb(n, d, rows=128):
-    return ("sbuf", [rows, n], d)
-
-
 _C = "float8_e4m3fn_x4"
-SCRATCH = {
-    "toh": _sb(8, "int32"), "xs": _sb(1024, "bfloat16"), "ws": _sb(1024, "bfloat16"),
-    "p8": _sb(16, "int32"), "Dc": _sb(48, "int32"), "kk": _sb(10, "int32"), "dupb": _sb(4, "int32"),
-    "R8r": _sb(144, "float32"), "R8": _sb(144, "float32"), "cvr": _sb(128, "float32"), "cval": _sb(128, "bfloat16"),
-    "idt": _sb(256, "bfloat16"), "Jr": _sb(144, "float32"), "J": _sb(144, "float32"), "J2r": _sb(18, "float32"),
-    "J2": _sb(18, "float32"), "c6": _sb(8, "float32"), "c6b": _sb(8, "float32"),
-    "p7i": _sb(8, "int32"), "b3": _sb(10, "int32"), "qi": _sb(4, "int32"), "h1": _sb(1, "int32"),
-    "repa": _sb(8, "uint16"), "repdi": _sb(10, "int32"), "repd": _sb(10, "uint16"), "dupi": _sb(4, "int32"),
-    "dup": _sb(4, "uint16"), "hf": _sb(1, "float32"), "qf": _sb(1, "float32"), "p7f": _sb(1, "float32"),
-    "p78f": _sb(1, "float32"), "lg": _sb(6, "uint16"), "tt3": _sb(10, "int32"), "rl": _sb(10, "uint16"),
-    "cb": _sb(48, "float32"), "zer": _sb(32, "float32"),
-    "dest": _sb(8, "int32"), "tou": _sb(8, "uint16"), "H": _sb(48, "float32"), "Cb": _sb(256, "float32"),
-    "Tr": _sb(32, "float32"), "QQ": _sb(64, "float32"), "Z": _sb(64, "float32"), "Sb": _sb(8, "bfloat16"),
-    "K": _sb(8, "float32"), "Xk": _sb(48, "float32"), "Xm": _sb(48, "float32"), "a1": _sb(24, "float32"),
-    "a2": _sb(8, "float32"), "P": _sb(8, "float32"), "Pu": _sb(8, "uint16"), "P6": _sb(8, "int32"),
-    "P48": _sb(8, "float32"), "T1": _sb(8, "float32"), "e1": _sb(8, "float32"), "off1": _sb(8, "uint16"),
-    "win1": _sb(288, "bfloat16"), "tr1": _sb(288, "bfloat16"),
-    "Y1": _sb(32, "float32"), "Yt1": _sb(32, "float32"), "Yd1": _sb(64, "float32"), "Z1": _sb(64, "float32"),
-    "l1": _sb(18, "uint16"), "l1o": _sb(4, "uint16"),
-    "Pf": _sb(128, "bfloat16"), "keywin": _sb(1536, "bfloat16"), "trk": _sb(1536, "bfloat16"),
-    "Xs": _sb(48, "bfloat16"), "Xin": _sb(48, "bfloat16"),
-    "cnt": _sb(64, "bfloat16"), "G": _sb(96, "float32"), "Nn": _sb(48, "float32"), "Lf": _sb(48, "int32"),
-    "Ai": _sb(48, "float32"), "off": _sb(48, "float32"), "FF": _sb(56, "int32"), "Bt": _sb(48, "float32"),
-    "U": _sb(48, "float32"), "Vv": _sb(48, "float32"), "DD": _sb(48, "float32"), "off2": _sb(8, "float32"),
-    "GE": _sb(144, "float32"), "M": _sb(144, "float32"), "Sm": _sb(144, "float32"), "lf": _sb(18, "float32"),
-    "l2": _sb(18, "uint16"), "l2o": _sb(4, "uint16"),
-    "P6x": _sb(48, "int32"), "tx": _sb(48, "float32"), "u6": _sb(48, "int32"), "mk": _sb(48, "float32"),
-    "V1": _sb(48, "float32"), "V2": _sb(48, "float32"), "V3": _sb(48, "float32"), "V4": _sb(48, "float32"),
-    "Wx": _sb(48, "float32"), "b1": _sb(24, "float32"), "b2": _sb(8, "float32"),
-    "Y2": _sb(32, "float32"), "Yt2": _sb(32, "float32"), "Yd2": _sb(64, "float32"), "Z2": _sb(64, "float32"),
-    "l3": _sb(16, "uint16"),
-    "qx": _sb(256, _C), "sx": _sb(256, "uint8"), "qw": _sb(256, _C), "sw": _sb(256, "uint8"),
-    "q1": _sb(288, _C), "s1": _sb(288, "uint8"), "land1": _sb(W1 + 1, _C), "lans1": _sb(W1 + 1, "uint8"),
-    "q2": _sb(288, _C), "s2": _sb(288, "uint8"), "land2": _sb(288, _C), "lans2": _sb(288, "uint8"),
-    "q3": _sb(256, _C), "s3": _sb(256, "uint8"),
-    "ps": ("psum", [128, 2048], "float32"), "ys": _sb(512, "float32"),
+_BUFS = {
+    "int32": "toh 8 p8 4 Dc 48 I4 4 tt3 9 dest 8 P6 8 Lf 48 FF 48 P6x 48 u6 48",
+    "uint16": "repa 4 repd 4 dup 4 lg 6 rl 10 tou 8 Pu 8 off1 8 l1 18 l1o 4 l2 18 l2o 4 l3 16",
+    "bfloat16": "xs 1024 ws 1024 cval 128 idt 256 Sb 8 win1 288 tr1 288 Pf 128 keywin 1536 trk 1536 Xs 48 Xin 48 cnt 64",
+    "float32": "R8r 144 R8 144 R8b 48 cvr 128 Jr 144 J2r 18 c6 8 F4 4 hf 1 cL 1 c1 1 kk 6 kkm 9 dupb 4 cb 48 zer 64 H 48 "
+               "Cb 256 Tr 64 QQ 64 Z 64 K 8 Xk 48 Xm 48 a1 24 a2 8 P 8 P48 8 T1 8 e1 8 Y1 32 Yt1 32 Yd1 64 Z1 64 G 96 Nn 48 "
+               "Ai 48 off 48 Bt 48 D 50 DD 48 off2 8 GE 144 M 144 Sm 144 lf 18 tx 48 mk 48 V1 48 V2 48 V3 48 "
+               "V4 48 Wx 48 b1 24 b2 8 Y2 32 Yt2 32 Yd2 64 Z2 64 ys 512",
+    _C: "qx 256 qw 256 q1 288 land1 264 q2 288 land2 288 q3 256",
+    "uint8": "sx 256 sw 256 s1 288 lans1 264 s2 288 lans2 288 s3 256",
 }
-SEMAPHORES = ["v", "gi1", "gi2", "to_in", "x_in", "w_in", "sb", "p_ok", "pf", "kz", "l1r", "l1own", "qxr", "q1c", "q1s",
-              "o1c", "o1s", "xsr", "xown", "cown", "l2r", "l2own", "q2c", "q2s", "o2c", "o2s", "l3r", "qwr",
-              "q3c0", "q3c1", "q3s0", "q3s1", "mm00", "mm01", "mm10", "mm11", "y0", "y1", "st",
-              "rc", "rx", "rc1", "rs1", "rc2", "rs2", "ls"]
+SCRATCH = {"ps": ("psum", [128, 2048], "float32")}
+for _d, _s in _BUFS.items():
+    _p = _s.split()
+    for _n, _w in zip(_p[0::2], _p[1::2]):
+        SCRATCH[_n] = ("sbuf", [128, int(_w)], _d)
+SEMAPHORES = ("v gi1 gi2 gi3 to_in x_in w_in zr ac sb p_ok pf kz l1r l1own qxr q1c q1s o1c o1s xsr xown cown l2r "
+              "l2own q2c q2s o2c o2s l3r qwr q3c0 q3c1 q3s0 q3s1 mm00 mm01 mm10 mm11 y0 y1 st "
+              "rc rx rc1 rs1 rc2 rs2 ls").split()
 
 
 def _shares(src, cores, topo, flip):
-    ds = [c for c in cores if c != src]
-    k = ds.index([c for c in cores + cores if c != src and cores.index(c) > cores.index(src)][0]) if src != cores[-1] else 0
-    ds = ds[k:] + ds[:k]
+    k = cores.index(src)
+    ds = cores[k + 1:] + cores[:k]
     ds = sorted(ds, key=lambda c: topo.die(c) == topo.die(src))
     e = topo.engines(src, ds[0])
     w = len(e) // 4
     if flip:
         e = e[w:] + e[:w]
-    out = {}
-    for i, c in enumerate(ds):
-        if i < 3:
-            out[c] = e[i * w:(i + 1) * w]
-        else:
-            h = w // 2
-            out[c] = e[3 * w + (i - 3) * h:3 * w + (i - 2) * h]
-    return out
+    h = w // 2
+    return {c: e[i * w:(i + 1) * w] if i < 3 else e[3 * w + (i - 3) * h:3 * w + (i - 2) * h] for i, c in enumerate(ds)}
 
 
 def rank_program(g, core, T, topo):
@@ -80,29 +45,62 @@ def rank_program(g, core, T, topo):
         return
     cores = list(T.cores)
     V, A, S, E = g.vector, g.scalar, g.sync, g.tensor
-    add, sub, mul = AluOpType.add, AluOpType.subtract, AluOpType.mult
-    mn, mx = AluOpType.min, AluOpType.max
-    eq, gt, le = AluOpType.is_equal, AluOpType.is_gt, AluOpType.is_le
-    shr, band = AluOpType.arith_shift_right, AluOpType.bitwise_and
-    Copy = ActivationFunctionType.Copy
-    tot = {}
+    O = AluOpType
+    add, sub, mul = O.add, O.subtract, O.mult
+    shr, band = O.arith_shift_right, O.bitwise_and
+    AF = ActivationFunctionType
+    tot, last, waited = {}, {}, {}
 
     def inc(inst, sem, n=1):
         inst.then_inc(T.sem[sem], n)
         tot[sem] = tot.get(sem, 0) + n
 
-    waited = [0]
-
-    def v(inst, sem="v"):
-        inc(inst, sem)
-
-    def vw():
-        if tot.get("v", 0) > waited[0]:
-            V.wait_ge(T.sem.v, tot["v"])
-            waited[0] = tot["v"]
+    def need(sem, n=None):
+        n = tot[sem] if n is None else n
+        if waited.get(sem, 0) < n:
+            waited[sem] = max(n, tot.get(sem, 0)) if sem == "v" else n
+            V.wait_ge(T.sem[sem], waited[sem])
 
     def w(q, sem, n):
         q.wait_ge(T.sem[sem], n)
+
+    def ap(s):
+        s, _, off = s.partition("@")
+        f = s.split(":")
+        a = T[f[0]][:, slice(*[int(i) for i in f[1:]])] if f[1:] else T[f[0]][:]
+        return a.indirect(ap(off)) if off else a
+
+    def reads(s):
+        for n in s.replace("@", ":").split(":"):
+            if n in last:
+                need(*last[n])
+
+    def v(call, out, ins, *more, sem="v"):
+        for s in ins + ([out] if "@" in out else []):
+            reads(s)
+        inc(call(ap(out), *[ap(s) for s in ins], *more), sem)
+        last[out.split(":")[0].split("@")[0]] = (sem, tot[sem])
+
+    def ts(out, i, s1, s2, *ops, **k):
+        for s in (s1, s2):
+            if isinstance(s, str):
+                reads(s)
+        v(V.tensor_scalar, out, [i], *[ap(s) if isinstance(s, str) else s for s in (s1, s2)], *ops, **k)
+
+    def tt(out, i, j, op, **k):
+        v(V.tensor_tensor, out, [i, j], op, **k)
+
+    def cp(out, i, **k):
+        v(V.tensor_copy, out, [i], **k)
+
+    def scan(out, i, j, op0, **k):
+        v(V.tensor_tensor_scan, out, [i, j], 0.0, op0, add, **k)
+
+    def tr(out, i):
+        v(V.transpose, out, [i])
+
+    def fill(s, c=0.0, **k):
+        v(V.memset, s, [], c, **k)
 
     def base1(r, m):
         return 0 if r == m else OWN + C1 * [k for k in range(N) if k != m].index(r)
@@ -112,269 +110,228 @@ def rank_program(g, core, T, topo):
 
     def fused(src_of, dst_of, sem, flip):
         sh = _shares(core, cores, topo, flip)
-        tr = []
+        t = []
         for c in sh:
             rid, pid, _ = topo.addr(c)
             d = cores.index(c)
-            tr.append(RemoteDMATransfer(dst_ids=[DstId(rid=rid, pnc=pid)], dma_engine_mask=sum(1 << e for e in sh[c]),
-                                        remote_sem=T.sem[sem], src=src_of(d), dst=dst_of(d)))
+            t.append(RemoteDMATransfer(dst_ids=[DstId(rid=rid, pnc=pid)], dma_engine_mask=sum(1 << e for e in sh[c]),
+                                       remote_sem=T.sem[sem], src=src_of(d), dst=dst_of(d)))
             tot["ls"] = tot.get("ls", 0) + len(sh[c])
-        g.remote_dma_fused(tr, local_sem=T.sem.ls)
+        g.remote_dma_fused(t, local_sem=T.sem.ls)
 
     for b in range(4):
-        for h in range(2):
-            q = S if h == 0 else A
-            inc(q.dma_start(T.toh[32 * b + 16 * h:32 * b + 16 * h + 16, :], T.to[:, 8 * h:8 * h + 8]), "to_in", 16)
+        inc((S, A)[b % 2].dma_start(T.toh[32 * b:32 * b + 32, :], T.to[:, :]), "to_in", 16)
     inc(S.dma_start(T.xs[:, 0:512], T.x[:, 0:512]), "x_in", 16)
     inc(A.dma_start(T.xs[:, 512:1024], T.x[:, 512:1024]), "x_in", 16)
-    inc(S.dma_start(T.ws[:, 0:1024], T.w[:, 0:1024]), "w_in", 16)
+    inc(S.dma_start(T.ws[:], T.w[:]), "w_in", 16)
 
-    inc(g.iota(T.p8[:], [[0, 16]], 0, 1), "gi1")
-    inc(g.iota(T.kk[:], [[2, 10]], 0, 0), "gi1")
-    inc(g.iota(T.dupb[:], [[16, 2], [0, 2]], 0, 0), "gi1")
-    inc(g.iota(T.Dc[:], [[1, 6], [0, 8]], 0, 0), "gi1")
-    inc(g.iota(T.R8r[:], [[0, 18], [1, 8]], 0, 0, allow_small_or_imprecise_dtypes=True), "gi1")
-    inc(g.iota(T.cvr[:], [[1, 128]], 0, 0, allow_small_or_imprecise_dtypes=True), "gi1")
-    inc(g.iota(T.idt[:], [[1, 256]], 1, 0, allow_small_or_imprecise_dtypes=True), "gi2")
-    inc(g.iota(T.c6[:], [[6, 8]], 0, 0, allow_small_or_imprecise_dtypes=True), "gi2")
-    inc(g.iota(T.J2r[:], [[0, 6], [16, 3]], 0, 0, allow_small_or_imprecise_dtypes=True), "gi2")
-    inc(g.iota(T.Jr[:], [[0, 6], [16, 3], [-1, 8]], 0, 0, allow_small_or_imprecise_dtypes=True), "gi2")
+    def iota(n, pat, sem, base=0, ch=0, **k):
+        inc(g.iota(ap(n), pat, base, ch, **k), sem)
 
-    v(V.memset(T.zer[:], 0.0))
-    v(V.memset(T.Cb[:, 48:256], 0.0))
-    v(V.memset(T.Sb[:], 0.0))
-    v(V.memset(T.Y1[:], 0.0))
-    v(V.memset(T.Y2[:], 0.0))
-    v(V.memset(T.win1[:], 0.0))
-    v(V.memset(T.cnt[:, 48:64], 0.0))
-    v(V.memset(T.FF[:], 0))
-    v(V.memset(T.cb[:], 0.0))
-    w(V, "gi1", tot["gi1"])
-    v(V.tensor_scalar(T.p7i[:], T.p8[:, 0:8], 7, None, band))
-    v(V.tensor_scalar(T.b3[:], T.p8[:, 0:10], 3, 1, shr, band))
-    v(V.tensor_scalar(T.qi[:], T.p8[:, 0:4], 15, None, band))
-    v(V.tensor_scalar(T.h1[:], T.p8[:, 0:1], 4, 1, shr, band))
-    v(V.tensor_scalar(T.R8[:], T.R8r[:], 1.0, None, mn))
-    vw()
-    v(V.tensor_copy(T.repa[:], T.p7i[:]))
-    v(V.tensor_tensor(T.repdi[:], T.b3[:], T.kk[:], add))
-    v(V.tensor_tensor(T.dupi[:], T.qi[:], T.dupb[:], add))
-    v(V.tensor_scalar(T.hf[:], T.h1[:], 128.0, None, mul))
-    v(V.tensor_copy(T.qf[:], T.qi[:, 0:1]))
-    v(V.tensor_copy(T.p7f[:], T.p7i[:, 0:1]))
-    v(V.tensor_scalar(T.p78f[:], T.p7i[:, 0:1], 8.0, None, mul))
-    for r in range(N):
-        d = base1(r, R) - r - (base1(r - 1, R) - (r - 1) if r else 0)
-        v(V.memset(T.cb[:, r:48:8], float(d)))
-    vw()
-    v(V.tensor_copy(T.repd[:], T.repdi[:]))
-    v(V.tensor_copy(T.dup[:], T.dupi[:]))
-    v(V.tensor_scalar(T.cval[:], T.cvr[:], T.hf[:, 0:1], None, add))
+    fl = {"allow_small_or_imprecise_dtypes": True}
+    iota("p8", [[0, 4]], "gi1", 0, 1)
+    iota("kk", [[1, 2], [2, 3]], "gi1", **fl)
+    iota("R8r", [[0, 18], [1, 8]], "gi1", **fl)
+    iota("dupb", [[16, 2], [0, 2]], "gi1", **fl)
+    iota("Dc", [[1, 6], [0, 8]], "gi2")
+    iota("cvr", [[16, 8], [1, 8], [128, 2]], "gi2", **fl)
+    iota("kkm", [[2, 9]], "gi2", -1, **fl)
+    iota("idt", [[1, 256]], "gi3", 1, **fl)
+    iota("c6", [[6, 8]], "gi3", -288, **fl)
+    iota("J2r", [[0, 6], [16, 3]], "gi3", **fl)
+    iota("Jr", [[0, 6], [16, 3], [-1, 8]], "gi3", **fl)
+    ng = dict(tot)
 
-    w(V, "to_in", tot["to_in"])
-    v(V.tensor_scalar(T.dest[:], T.toh[:], 8, None, shr))
-    vw()
-    v(V.tensor_tensor(T.H[:], T.dest[:, 0:8].indirect(T.repa[:, 0:3]), T.Dc[:], eq))
-    vw()
-    v(V.tensor_tensor_scan(T.Cb[:, 0:48], T.R8[:, 0:48], T.H[:], 0.0, mul, add))
-    vw()
-    v(V.transpose(T.Tr[:], T.Cb[:, 7:256:8]))
-    vw()
-    v(V.tensor_tensor_scan(T.QQ[:, 0:32], T.Tr[:], T.zer[:], 0.0, add, add))
-    vw()
-    v(V.tensor_scalar(T.QQ[:, 32:64], T.zer[:], T.QQ[:, 31:32], None, add))
-    vw()
-    v(V.transpose(T.Z[:], T.QQ[:]))
-    vw()
-    v(V.tensor_tensor_scan(T.Sb[:, 1:7], T.Z[:, 32:38], T.zer[:, 0:6], 0.0, add, add), "sb")
-    w(V, "sb", 1)
-    v(V.tensor_tensor(T.K[:, 0:6], T.Z[:, 0:6], T.Sb[:, 0:6], add))
-    vw()
-    v(V.tensor_tensor(T.Xk[:], T.K[:, 0:6].indirect(T.repd[:, 0:3]), T.Cb[:, 0:48], sub))
-    vw()
-    v(V.tensor_tensor(T.Xm[:], T.Xk[:], T.H[:], mul))
-    vw()
-    v(V.tensor_tensor(T.a1[:], T.Xm[:, 0:24], T.Xm[:, 24:48], add))
-    vw()
-    v(V.tensor_tensor(T.a2[:], T.a1[:, 0:8], T.a1[:, 8:16], add))
-    vw()
-    v(V.tensor_tensor(T.P[:], T.a2[:], T.a1[:, 16:24], add))
-    vw()
-    v(V.tensor_scalar(T.P6[:], T.P[:], 1.0 / 6, -2.5 / 6, mul, add))
-    v(V.tensor_scalar(T.P48[:], T.P[:], 48.0, None, mul))
-    v(V.tensor_copy(T.Pu[:], T.P[:]), "p_ok")
-    vw()
-    v(V.tensor_scalar(T.T1[:], T.P6[:], -287.0, None, mul))
-    vw()
-    v(V.tensor_tensor(T.e1[:], T.T1[:], T.P48[:], add))
-    vw()
-    v(V.tensor_copy(T.off1[:], T.e1[:]))
-    w(V, "x_in", tot["x_in"])
-    v(V.quantize_mx(T.qx[:], T.sx[:], T.xs[:]), "qxr")
-    vw()
-    v(V.tensor_copy(T.win1[:, 0:288].indirect(T.off1[:, 0:8]), T.cval[:]))
-    vw()
-    v(V.transpose(T.tr1[:], T.win1[:]))
-    vw()
+    fill("zer", sem="zr")
+    fill("Sb")
+    fill("win1")
+    fill("Tr:32:64")
+    fill("Cb:48:256")
+    need("gi1", ng["gi1"])
+    ts("I4:0:1", "p8:0:1", 7, None, band)
+    ts("I4:1:2", "p8:1:2", 3, 1, shr, band)
+    ts("I4:2:3", "p8:2:3", 15, None, band)
+    ts("I4:3:4", "p8:3:4", 4, 1, shr, band)
+    ts("R8", "R8r", 1.0, None, O.min)
+    cp("F4", "I4")
+    ts("repa:0:3", "zer:0:3", "F4:0:1", None, add)
+    ts("repd:0:3", "kk:0:3", "F4:1:2", None, add)
+    ts("dup", "dupb", "F4:2:3", None, add)
+    ts("hf", "F4:3:4", 8.0, None, mul)
+    ts("c1", "F4:0:1", 8.0, "F4:1:2", mul, add)
+    ts("cL", "F4:2:3", -1.0, (2.5 - R) / 6, mul, add)
+    need("gi2", ng["gi2"])
+    ts("cval", "cvr", "hf", None, add)
+    ts("tt3", "kkm", "F4:1:2", 1.0 / 3, add, mul)
+    ts("lg", "kk", "c1", None, add)
+    fill("Y1")
 
-    def across(Y, Yt, Yd, Zz, lst, nb, sem):
-        v(V.transpose(Yt[:], Y[:]))
-        vw()
-        v(V.tensor_copy(Yd[:], Yt[:].indirect(T.dup[:, 0:4])))
-        vw()
-        v(V.transpose(Zz[:], Yd[:]))
-        vw()
-        v(V.tensor_copy(lst[:, 0:2 * nb:2], Zz[:, 0:nb]), sem)
-        v(V.tensor_copy(lst[:, 1:2 * nb:2], Zz[:, 32:32 + nb]), sem)
-        w(V, sem, 2)
+    need("to_in")
+    ts("dest", "toh", 8, None, shr)
+    cp("tou", "toh")
+    tt("H", "dest:0:8@repa:0:3", "Dc", O.is_equal)
+    ts("rl:0:9", "tt3", 8.0, "F4:0:1", mul, add)
+    scan("Cb:0:48", "R8:0:48", "H", mul)
+    tr("Tr:0:32", "Cb:7:256:8")
+    scan("QQ", "Tr", "zer", add)
+    cp("R8b", "R8:0:48")
+    tr("Z", "QQ")
+    scan("Sb:1:7", "Z:32:38", "zer:0:6", add, sem="sb")
+    tt("K:0:6", "Z:0:6", "Sb:0:6", add)
+    fill("R8b:7:48:8")
+    tt("Xk", "K:0:6@repd:0:3", "Cb:0:48", sub)
+    tt("Xm", "Xk", "H", mul)
+    tt("a1", "Xm:0:24", "Xm:24:48", add)
+    tt("a2", "a1:0:8", "a1:8:16", add)
+    tt("P", "a2", "a1:16:24", add)
+    ts("P6", "P", 1.0 / 6, -2.5 / 6, mul, add)
+    ts("P48", "P", 48.0, None, mul)
+    cp("Pu", "P", sem="p_ok")
+    ts("T1", "P6", -287.0, None, mul)
+    tt("e1", "T1", "P48", add)
+    cp("off1", "e1")
+    need("x_in")
+    v(V.quantize_mx, "qx", [], T.sx[:], T.xs[:], sem="qxr")
+    cp("win1:0:288@off1:0:8", "cval")
+    tr("tr1", "win1")
 
-    v(V.tensor_tensor(T.Y1[:, 0:9], T.tr1[:, 0:288:32], T.tr1[:, 16:288:32], add))
-    vw()
-    across(T.Y1, T.Yt1, T.Yd1, T.Z1, T.l1, 9, "l1r")
-    w(V, "qxr", 1)
+    def across(k, lst, nb, sem):
+        tr("Yt" + k, "Y" + k)
+        cp("Yd" + k, "Yt%s:0:32@dup:0:4" % k)
+        tr("Z" + k, "Yd" + k)
+        cp("%s:0:%d:2" % (lst, 2 * nb), "Z%s:0:%d" % (k, nb), sem=sem)
+        cp("%s:1:%d:2" % (lst, 2 * nb), "Z%s:32:%d" % (k, 32 + nb), sem=sem)
+        need(sem)
 
-    def pickc(out, a, b, src, n, lst, c, e):
-        return V.tensor_copy(out[:, a:b].bitcast(dt.uint32), src[:, 0:n].bitcast(dt.uint32).indirect(lst[:, c:e]))
+    tt("Y1:0:9", "tr1:0:288:32", "tr1:16:288:32", add)
+    across("1", "l1", 9, "l1r")
+    need("qxr")
 
-    def picks(out, a, b, src, n, lst, c, e):
-        return A.activation(out[:, a:b], src[:, 0:n].indirect(lst[:, c:e]), Copy)
+    def pickc(out, a, b, src, n, lst, c, e, sem):
+        inc(V.tensor_copy(T[out][:, a:b].bitcast(dt.uint32), T[src][:, 0:n].bitcast(dt.uint32).indirect(T[lst][:, c:e])), sem)
 
-    v(pickc(T.q1, 0, 288, T.qx, 256, T.l1, 0, 18), "q1c")
-    v(V.tensor_copy(T.l1o[:, 0:3], T.l1[:, 3 * R:3 * R + 3]), "l1own")
-    w(V, "l1own", 1)
-    v(pickc(T.land1, 0, 48, T.qx, 256, T.l1o, 0, 3), "o1c")
+    def picks(out, a, b, src, n, lst, c, e, sem):
+        inc(A.activation(T[out][:, a:b], T[src][:, 0:n].indirect(T[lst][:, c:e]), AF.Copy), sem)
 
-    w(V, "pf", 1)
-    w(V, "kz", 2)
-    v(V.tensor_copy(T.tou[:], T.toh[:]))
-    vw()
-    v(V.tensor_copy(T.keywin[:].indirect(T.tou[:, 0:8]), T.Pf[:]))
-    vw()
-    v(V.transpose(T.trk[:], T.keywin[:]))
-    vw()
-    v(V.tensor_tensor(T.Xs[:], T.trk[:, 0:1536:32], T.trk[:, 16:1536:32], add), "xsr")
+    pickc("q1", 0, 288, "qx", 256, "l1", 0, 18, "q1c")
 
-    w(V, "gi2", tot["gi2"])
-    v(V.tensor_scalar(T.lg[:, 0:3], T.repdi[:, 0:3], T.p78f[:, 0:1], None, add))
-    v(V.tensor_scalar(T.lg[:, 3:6], T.repdi[:, 0:3], T.p78f[:, 0:1], 1.0, add, add))
-    v(V.tensor_scalar(T.tt3[:], T.repdi[:], 1.0 / 3, -1.0 / 3, mul, add))
-    v(V.tensor_scalar(T.J[:], T.Jr[:], T.qf[:, 0:1], None, add))
-    v(V.tensor_scalar(T.J2[:], T.J2r[:], T.qf[:, 0:1], None, add))
-    v(V.tensor_scalar(T.c6b[:], T.c6[:], -291.5, None, add))
-    vw()
-    v(V.tensor_scalar(T.rl[:], T.tt3[:], 8.0, T.p7f[:, 0:1], mul, add))
+    need("pf", 1)
+    need("kz", 2)
+    cp("keywin:0:1536@tou:0:8", "Pf")
+    cp("l1o:0:3", "l1:%d:%d" % (3 * R, 3 * R + 3), sem="l1own")
+    tr("trk", "keywin")
+    need("l1own")
+    pickc("land1", 0, 48, "qx", 256, "l1o", 0, 3, "o1c")
+    tt("Xs", "trk:0:1536:32", "trk:16:1536:32", add, sem="xsr")
+
+    need("gi3", ng["gi3"])
+    need("ac", 11)
     nr = arrivals(False)
-    w(V, "rc", nr)
-    w(V, "cown", 1)
-    v(V.tensor_copy(T.G[:], T.cnt[:, 0:64].indirect(T.lg[:, 0:6])))
-    vw()
-    v(V.tensor_tensor(T.Nn[:], T.G[:, 48:96], T.G[:, 0:48], sub))
-    v(V.tensor_scalar(T.Lf[:], T.G[:, 0:48], 1.0 / 6, (5 - R) / 6 - 2.5 / 6, mul, add))
-    vw()
-    v(V.tensor_tensor_scan(T.Ai[:], T.R8[:, 0:48], T.Nn[:], 0.0, mul, add))
-    vw()
-    v(V.tensor_tensor(T.off[:], T.Ai[:], T.G[:, 48:96], sub))
-    vw()
-    v(V.tensor_scalar(T.FF[:, 1:49], T.off[:], 1.0 / 6, R / 6 - 2.5 / 6, mul, add))
-    v(V.tensor_tensor(T.off2[:, 0:6], T.off[:, 8 * R:8 * R + 6], T.c6b[:, 0:6], add))
-    vw()
-    v(V.tensor_tensor(T.Bt[:], T.Lf[:], T.FF[:, 1:49], add))
-    v(V.tensor_tensor(T.U[:], T.FF[:, 0:48], T.R8[:, 0:48], mul))
-    v(V.tensor_tensor(T.Vv[:], T.cb[:], T.FF[:, 1:49], sub))
-    vw()
-    v(V.tensor_tensor(T.GE[:], T.Bt[:].indirect(T.rl[:, 0:9]), T.J[:], le))
-    v(V.tensor_tensor(T.DD[:], T.U[:], T.Vv[:], add))
-    vw()
-    v(V.tensor_tensor(T.M[:], T.DD[:].indirect(T.rl[:, 0:9]), T.GE[:], mul))
-    vw()
-    v(V.tensor_tensor_scan(T.Sm[:], T.R8[:], T.M[:], 0.0, mul, add))
-    vw()
-    v(V.tensor_tensor(T.lf[:], T.Sm[:, 5:144:8], T.J2[:], add))
-    vw()
-    v(V.tensor_scalar(T.l2[:], T.lf[:], 0.0, float(W1 - 1), mx, mn), "l2r")
-    v(V.tensor_scalar(T.l2o[:, 0:3], T.lf[:, 3 * R:3 * R + 3], 0.0, float(W1 - 1), mx, mn), "l2own")
-    w(V, "l2r", 1)
-    w(V, "o1c", 1)
-    w(V, "rc1", arrivals(False))
-    v(pickc(T.q2, 0, 288, T.land1, W1, T.l2, 0, 18), "q2c")
-    w(V, "l2own", 1)
-    v(pickc(T.land2, 48 * R, 48 * R + 48, T.land1, W1, T.l2o, 0, 3), "o2c")
-    w(V, "w_in", tot["w_in"])
-    v(V.quantize_mx(T.qw[:], T.sw[:], T.ws[:]), "qwr")
+    need("rc", nr)
+    need("cown", 1)
+    cp("G", "cnt:0:64@lg:0:6")
+    tt("Nn", "G:48:96", "G:0:48", sub)
+    ts("Lf", "G:0:48", 1.0 / 6, "cL", mul, add)
+    scan("Ai", "R8b", "Nn", mul)
+    tt("off", "Ai", "G:48:96", sub)
+    ts("FF", "off", 1.0 / 6, R / 6 - 2.5 / 6, mul, add)
+    tt("off2:0:6", "off:%d:%d" % (8 * R, 8 * R + 6), "c6:0:6", add)
+    tt("D:1:49", "cb", "FF", sub)
+    tt("Bt", "Lf", "FF", add)
+    tt("DD", "D:1:49", "D:0:48", sub)
+    tt("GE", "Bt:0:48@rl:0:9", "Jr", O.is_le)
+    tt("M", "DD:0:48@rl:0:9", "GE", mul)
+    scan("Sm", "R8", "M", mul)
+    tt("lf", "Sm:5:144:8", "J2r", add)
+    ts("l2", "lf", "F4:2:3", float(W1 - 1), add, O.min, sem="l2r")
+    ts("l2o:0:3", "lf:%d:%d" % (3 * R, 3 * R + 3), "F4:2:3", float(W1 - 1), add, O.min, sem="l2own")
+    need("l2r")
+    need("o1c")
+    need("rc1", arrivals(False))
+    pickc("q2", 0, 288, "land1", W1, "l2", 0, 18, "q2c")
+    need("l2own")
+    pickc("land2", 48 * R, 48 * R + 48, "land1", W1, "l2o", 0, 3, "o2c")
+    need("w_in")
+    v(V.quantize_mx, "qw", [], T.sw[:], T.ws[:], sem="qwr")
 
-    w(V, "rx", nr)
-    w(V, "xown", 1)
-    v(V.tensor_scalar(T.P6x[:], T.Xin[:], 1.0 / 6, -3.5 / 6, mul, add))
-    v(V.tensor_tensor(T.tx[:], T.off2[:, 0:6].indirect(T.repd[:, 0:3]), T.Xin[:], add))
-    v(V.tensor_scalar(T.mk[:], T.Xin[:], 0.0, None, gt))
-    v(V.tensor_scalar(T.Wx[:], T.Xin[:], 48.0, None, mul))
-    vw()
-    v(V.tensor_scalar(T.V1[:], T.P6x[:], -288.0, None, mul))
-    v(V.tensor_scalar(T.u6[:], T.tx[:], 1.0 / 6, None, mul))
-    vw()
-    v(V.tensor_tensor(T.V2[:], T.V1[:], T.Wx[:], add))
-    vw()
-    v(V.tensor_tensor(T.V3[:], T.V2[:], T.u6[:], add))
-    vw()
-    v(V.tensor_tensor(T.V4[:], T.V3[:], T.mk[:], mul))
-    vw()
-    v(V.tensor_tensor(T.b1[:], T.V4[:, 0:24], T.V4[:, 24:48], add))
-    vw()
-    v(V.tensor_tensor(T.b2[:], T.b1[:, 0:8], T.b1[:, 8:16], add))
-    vw()
-    v(V.tensor_tensor(T.Y2[:, 0:8], T.b2[:], T.b1[:, 16:24], add))
-    vw()
-    across(T.Y2, T.Yt2, T.Yd2, T.Z2, T.l3, 8, "l3r")
-    w(V, "o2c", 1)
-    w(V, "rc2", arrivals(False))
+    need("rx", nr)
+    need("xown", 1)
+    ts("P6x", "Xin", 1.0 / 6, -3.5 / 6, mul, add)
+    tt("tx", "off2:0:6@repd:0:3", "Xin", add)
+    ts("mk", "Xin", 0.0, None, O.is_gt)
+    ts("Wx", "Xin", 48.0, None, mul)
+    ts("V1", "P6x", -288.0, None, mul)
+    ts("u6", "tx", 1.0 / 6, -3.5 / 6, mul, add)
+    tt("V2", "V1", "Wx", add)
+    tt("V3", "V2", "u6", add)
+    tt("V4", "V3", "mk", mul)
+    tt("b1", "V4:0:24", "V4:24:48", add)
+    tt("b2", "b1:0:8", "b1:8:16", add)
+    tt("Y2:0:8", "b2", "b1:16:24", add)
+    across("2", "l3", 8, "l3r")
+    need("o2c")
+    need("rc2", arrivals(False))
     for h in range(2):
-        v(pickc(T.q3, 128 * h, 128 * h + 128, T.land2, 288, T.l3, 8 * h, 8 * h + 8), "q3c%d" % h)
+        pickc("q3", 128 * h, 128 * h + 128, "land2", 288, "l3", 8 * h, 8 * h + 8, "q3c%d" % h)
+
+    def part(o, h):
+        return slice(256 * o + 128 * h, 256 * o + 128 * h + 128), slice(512 * (2 * o + h), 512 * (2 * o + h) + 128)
+
     for h in range(2):
-        w(V, "mm0%d" % h, 1)
-        v(V.tensor_copy(T.ys[:, 128 * h:128 * h + 128], T.ps[:, 512 * h:512 * h + 128]), "y0")
+        y, p = part(0, h)
+        need("mm0%d" % h, 1)
+        inc(V.tensor_copy(T.ys[:, y], T.ps[:, p]), "y0")
 
     w(E, "qwr", 1)
     for h in range(2):
         w(E, "q3c%d" % h, 1)
         w(E, "q3s%d" % h, 1)
         for o in range(2):
-            b = 512 * (2 * o + h)
-            inc(E.matmul_mx(T.ps[:, b:b + 128], T.qw[:, 128 * o:128 * o + 128], T.sw[:, 128 * o:128 * o + 128],
+            inc(E.matmul_mx(T.ps[:, part(o, h)[1]], T.qw[:, 128 * o:128 * o + 128], T.sw[:, 128 * o:128 * o + 128],
                             T.q3[:, 128 * h:128 * h + 128], T.s3[:, 128 * h:128 * h + 128], True, True), "mm%d%d" % (o, h))
 
+    def act(out, i, sem, f=AF.Copy, **k):
+        inc(A.activation(ap(out), ap(i), f, **k), sem)
+
+    w(A, "zr", 1)
+    for r in range(8):
+        act("cb:%d:48:8" % r, "zer:0:6", "ac", bias=float(base1(r, R) - r) if r < N else 0.0)
+    act("Y2", "zer:0:32", "ac")
+    act("D:0:1", "zer:0:1", "ac")
+    act("cnt:48:64", "zer:0:16", "ac")
     w(A, "x_in", tot["x_in"])
-    inc(A.activation(T.keywin[:, 0:1024], T.xs[:, 0:1024], Copy, scale=0.0), "kz")
-    inc(A.activation(T.keywin[:, 1024:1536], T.xs[:, 0:512], Copy, scale=0.0), "kz")
+    act("keywin:0:1024", "xs", "kz", scale=0.0)
+    act("keywin:1024:1536", "xs:0:512", "kz", scale=0.0)
     w(A, "sb", 1)
-    inc(A.activation(T.cnt[:, 8 * R:8 * R + 8], T.Sb[:], Copy), "cown")
+    act("cnt:%d:%d" % (8 * R, 8 * R + 8), "Sb", "cown")
+    w(A, "gi3", ng["gi3"])
     w(A, "p_ok", 1)
-    w(A, "gi2", tot["gi2"])
-    inc(A.activation(T.Pf[:], T.idt[:, 0:256].indirect(T.Pu[:, 0:8]), Copy), "pf")
+    act("Pf", "idt:0:256@Pu:0:8", "pf")
     w(A, "qxr", 1)
     w(A, "l1r", 2)
-    inc(picks(T.s1, 0, 288, T.sx, 256, T.l1, 0, 18), "q1s")
+    picks("s1", 0, 288, "sx", 256, "l1", 0, 18, "q1s")
     w(A, "l1own", 1)
-    inc(picks(T.lans1, 0, 48, T.sx, 256, T.l1o, 0, 3), "o1s")
+    picks("lans1", 0, 48, "sx", 256, "l1o", 0, 3, "o1s")
     w(A, "xsr", 1)
-    inc(A.activation(T.Xin[:, 8 * R:8 * R + 8], T.Xs[:, 8 * R:8 * R + 8], Copy), "xown")
+    act("Xin:%d:%d" % (8 * R, 8 * R + 8), "Xs:%d:%d" % (8 * R, 8 * R + 8), "xown")
     w(A, "l2r", 1)
     w(A, "o1s", 1)
     w(A, "rs1", arrivals(True))
-    inc(picks(T.s2, 0, 288, T.lans1, W1, T.l2, 0, 18), "q2s")
+    picks("s2", 0, 288, "lans1", W1, "l2", 0, 18, "q2s")
     w(A, "l2own", 1)
-    inc(picks(T.lans2, 48 * R, 48 * R + 48, T.lans1, W1, T.l2o, 0, 3), "o2s")
+    picks("lans2", 48 * R, 48 * R + 48, "lans1", W1, "l2o", 0, 3, "o2s")
     w(A, "l3r", 2)
     w(A, "o2s", 1)
     w(A, "rs2", arrivals(True))
     for h in range(2):
-        inc(picks(T.s3, 128 * h, 128 * h + 128, T.lans2, 288, T.l3, 8 * h, 8 * h + 8), "q3s%d" % h)
+        picks("s3", 128 * h, 128 * h + 128, "lans2", 288, "l3", 8 * h, 8 * h + 8, "q3s%d" % h)
     for h in range(2):
+        y, p = part(1, h)
         w(A, "mm1%d" % h, 1)
-        inc(A.activation(T.ys[:, 256 + 128 * h:384 + 128 * h], T.ps[:, 1024 + 512 * h:1152 + 512 * h], Copy), "y1")
-    w(A, "y1", 2)
-    inc(A.dma_start(T.y[:, 256:512], T.ys[:, 256:512]), "st", 16)
-    w(S, "y0", 2)
-    inc(S.dma_start(T.y[:, 0:256], T.ys[:, 0:256]), "st", 16)
+        inc(A.activation(T.ys[:, y], T.ps[:, p], AF.Copy), "y1")
+    for q, o in ((S, 0), (A, 1)):
+        w(q, "y%d" % o, 2)
+        inc(q.dma_start(T.y[:, 256 * o:256 * o + 256], T.ys[:, 256 * o:256 * o + 256]), "st", 16)
 
     w(g, "sb", 1)
     fused(lambda d: T.Sb[:, 0:8], lambda d: T.cnt[:, 8 * R:8 * R + 8], "rc", False)

@@ -3,27 +3,27 @@ from concourse.mybir import dt, AluOpType, ActivationFunctionType
 
 N = 6
 C1, C2 = 43, 48
-OWN = 48
-W1 = OWN + 5 * C1
+OUT = 6 * 48
+W1 = OUT + 5 * C1
 _C = "float8_e4m3fn_x4"
 _BUFS = {
-    "int32": "toh 8 p8 4 Dc 48 I4 4 tt3 9 dest 8 P6 8 Lf 48 FF 48 P6x 48 u6 48",
-    "uint16": "repa 4 repd 4 dup 4 lg 6 rl 10 tou 8 Pu 8 off1 8 l1 18 l1o 4 l2 18 l2o 4 l3 16",
+    "int32": "toh 8 p8 4 Dc 48 Dc2 64 I4 4 tt3 9 dest 8 P6 8 Lf 48 FF 48 P6x 48 u6 48",
+    "uint16": "repa 4 repd 4 pm 4 dup 4 lg 6 rl 10 tou 8 Pu 8 off1 8 l1 18 l2 18 l2o 4 l3 16",
     "bfloat16": "xs 1024 ws 1024 cval 128 idt 256 Sb 8 win1 288 tr1 288 Pf 128 keywin 1536 trk 1536 Xs 48 Xin 48 cnt 64",
-    "float32": "R8r 144 R8 144 R8b 48 cvr 128 Jr 144 J2r 18 c6 8 F4 4 hf 1 cL 1 c1 1 kk 6 kkm 9 dupb 4 cb 48 zer 64 H 48 "
-               "Cb 256 Tr 64 QQ 64 Z 64 K 8 Xk 48 Xm 48 a1 24 a2 8 P 8 P48 8 T1 8 e1 8 Y1 32 Yt1 32 Yd1 64 Z1 64 G 96 Nn 48 "
-               "Ai 48 off 48 Bt 48 D 50 DD 48 off2 8 GE 144 M 144 Sm 144 lf 18 tx 48 mk 48 V1 48 V2 48 V3 48 "
+    "float32": "R8 64 R8L 144 cvr 128 Jr 144 J2r 18 c6 8 F4 4 hf 1 cL 1 c1 1 kk 6 kk4 4 kkm 9 dupb 4 cb 48 zer 32 LE 48 "
+               "H2 64 Cb 264 Cd 48 B3 96 QQ 64 Z 64 K 8 Xk 64 Xm 64 PP 64 P48 8 T1 8 e1 8 Y1 32 Yt1 32 Yd1 64 Z1 64 G 96 "
+               "off 48 Bt 48 D 50 DD 48 off2 8 GE 144 M 144 Sm 144 lf 18 tx 48 mk 48 V1 48 V2 48 V3 48 "
                "V4 48 Wx 48 b1 24 b2 8 Y2 32 Yt2 32 Yd2 64 Z2 64 ys 512",
-    _C: "qx 256 qw 256 q1 288 land1 264 q2 288 land2 288 q3 256",
-    "uint8": "sx 256 sw 256 s1 288 lans1 264 s2 288 lans2 288 s3 256",
+    _C: "qx 256 qw 256 land1 512 q2 288 land2 288 q3 256",
+    "uint8": "sx 256 sw 256 lans1 512 s2 288 lans2 288 s3 256",
 }
 SCRATCH = {"ps": ("psum", [128, 2048], "float32")}
 for _d, _s in _BUFS.items():
     _p = _s.split()
     for _n, _w in zip(_p[0::2], _p[1::2]):
         SCRATCH[_n] = ("sbuf", [128, int(_w)], _d)
-SEMAPHORES = ("v gi1 gi2 gi3 to_in x_in w_in zr ac sb p_ok pf kz l1r l1own qxr q1c q1s o1c o1s xsr xown cown l2r "
-              "l2own q2c q2s o2c o2s l3r qwr q3c0 q3c1 q3s0 q3s1 mm00 mm01 mm10 mm11 y0 y1 st "
+SEMAPHORES = ("v gi1 gi2 gi3 to_in x_in w_in zr r8 ac sb p_ok pf kz l1r qxr q1c q1s xsr xown cown l2r "
+              "l2own q2c q2s o2c o2s l3r qwr q3c0 q3c1 q3s0 q3s1 mm00 mm01 mm10 mm11 y00 y01 y10 y11 st "
               "rc rx rc1 rs1 rc2 rs2 ls").split()
 
 
@@ -32,11 +32,10 @@ def _shares(src, cores, topo, flip):
     ds = cores[k + 1:] + cores[:k]
     ds = sorted(ds, key=lambda c: topo.die(c) == topo.die(src))
     e = topo.engines(src, ds[0])
-    w = len(e) // 4
+    h, w = len(e) // 2, len(e) // 8
     if flip:
-        e = e[w:] + e[:w]
-    h = w // 2
-    return {c: e[i * w:(i + 1) * w] if i < 3 else e[3 * w + (i - 3) * h:3 * w + (i - 2) * h] for i, c in enumerate(ds)}
+        e = e[h:] + e[:h]
+    return {c: e[:h] if i == 0 else e[h + (i - 1) * w:h + i * w] for i, c in enumerate(ds)}
 
 
 def rank_program(g, core, T, topo):
@@ -93,8 +92,8 @@ def rank_program(g, core, T, topo):
     def cp(out, i, **k):
         v(V.tensor_copy, out, [i], **k)
 
-    def scan(out, i, j, op0, **k):
-        v(V.tensor_tensor_scan, out, [i, j], 0.0, op0, add, **k)
+    def scan(out, i, j, op0, op1=O.add, **k):
+        v(V.tensor_tensor_scan, out, [i, j], 0.0, op0, op1, **k)
 
     def tr(out, i):
         v(V.transpose, out, [i])
@@ -103,7 +102,7 @@ def rank_program(g, core, T, topo):
         v(V.memset, s, [], c, **k)
 
     def base1(r, m):
-        return 0 if r == m else OWN + C1 * [k for k in range(N) if k != m].index(r)
+        return 48 * m if r == m else OUT + C1 * [k for k in range(N) if k != m].index(r)
 
     def arrivals(flip):
         return sum(len(_shares(c, cores, topo, flip)[core]) for c in cores if c != core)
@@ -130,69 +129,71 @@ def rank_program(g, core, T, topo):
 
     fl = {"allow_small_or_imprecise_dtypes": True}
     iota("p8", [[0, 4]], "gi1", 0, 1)
-    iota("kk", [[1, 2], [2, 3]], "gi1", **fl)
-    iota("R8r", [[0, 18], [1, 8]], "gi1", **fl)
+    iota("kk4", [[2, 4]], "gi1", **fl)
+    iota("Dc2", [[0, 8], [1, 8]], "gi1")
     iota("dupb", [[16, 2], [0, 2]], "gi1", **fl)
-    iota("Dc", [[1, 6], [0, 8]], "gi2")
+    iota("Dc", [[256, 6], [0, 8]], "gi2", 256)
     iota("cvr", [[16, 8], [1, 8], [128, 2]], "gi2", **fl)
+    iota("kk", [[1, 2], [2, 3]], "gi2", **fl)
     iota("kkm", [[2, 9]], "gi2", -1, **fl)
     iota("idt", [[1, 256]], "gi3", 1, **fl)
     iota("c6", [[6, 8]], "gi3", -288, **fl)
     iota("J2r", [[0, 6], [16, 3]], "gi3", **fl)
     iota("Jr", [[0, 6], [16, 3], [-1, 8]], "gi3", **fl)
+    iota("cnt:48:56", [[-256, 8]], "gi3", **fl)
     ng = dict(tot)
 
     fill("zer", sem="zr")
     fill("Sb")
     fill("win1")
-    fill("Tr:32:64")
-    fill("Cb:48:256")
+    fill("B3")
+    fill("Cb")
     need("gi1", ng["gi1"])
     ts("I4:0:1", "p8:0:1", 7, None, band)
     ts("I4:1:2", "p8:1:2", 3, 1, shr, band)
     ts("I4:2:3", "p8:2:3", 15, None, band)
     ts("I4:3:4", "p8:3:4", 4, 1, shr, band)
-    ts("R8", "R8r", 1.0, None, O.min)
+    ts("R8", "Dc2", 1.0, None, O.min, sem="r8")
     cp("F4", "I4")
+    fill("Xk:48:64")
     ts("repa:0:3", "zer:0:3", "F4:0:1", None, add)
-    ts("repd:0:3", "kk:0:3", "F4:1:2", None, add)
+    ts("repd", "kk4", "F4:1:2", None, add)
     ts("dup", "dupb", "F4:2:3", None, add)
     ts("hf", "F4:3:4", 8.0, None, mul)
     ts("c1", "F4:0:1", 8.0, "F4:1:2", mul, add)
     ts("cL", "F4:2:3", -1.0, (2.5 - R) / 6, mul, add)
     need("gi2", ng["gi2"])
     ts("cval", "cvr", "hf", None, add)
+    ts("pm", "kk4", "c1", None, add)
     ts("tt3", "kkm", "F4:1:2", 1.0 / 3, add, mul)
     ts("lg", "kk", "c1", None, add)
-    fill("Y1")
 
     need("to_in")
+    tt("LE", "toh:0:8@repa:0:3", "Dc", O.is_lt)
     ts("dest", "toh", 8, None, shr)
+    scan("Cb:8:56", "R8:0:48", "LE", mul)
     cp("tou", "toh")
-    tt("H", "dest:0:8@repa:0:3", "Dc", O.is_equal)
+    tr("B3:32:64", "Cb:15:264:8")
+    tt("H2", "dest:0:8@repd", "Dc2", O.is_equal)
+    scan("QQ", "B3:32:96", "B3:0:64", add, sub)
     ts("rl:0:9", "tt3", 8.0, "F4:0:1", mul, add)
-    scan("Cb:0:48", "R8:0:48", "H", mul)
-    tr("Tr:0:32", "Cb:7:256:8")
-    scan("QQ", "Tr", "zer", add)
-    cp("R8b", "R8:0:48")
     tr("Z", "QQ")
-    scan("Sb:1:7", "Z:32:38", "zer:0:6", add, sem="sb")
-    tt("K:0:6", "Z:0:6", "Sb:0:6", add)
-    fill("R8b:7:48:8")
-    tt("Xk", "K:0:6@repd:0:3", "Cb:0:48", sub)
-    tt("Xm", "Xk", "H", mul)
-    tt("a1", "Xm:0:24", "Xm:24:48", add)
-    tt("a2", "a1:0:8", "a1:8:16", add)
-    tt("P", "a2", "a1:16:24", add)
-    ts("P6", "P", 1.0 / 6, -2.5 / 6, mul, add)
-    ts("P48", "P", 48.0, None, mul)
-    cp("Pu", "P", sem="p_ok")
+    tt("Cd", "Cb:8:56", "Cb:0:48", sub)
+    tt("K:0:6", "Z:0:6", "Z:31:37", add)
+    tt("Sb:1:7", "Z:0:6", "Z:32:38", add, sem="sb")
+    tt("Xk:0:48", "K:0:6@repd:0:3", "Cd", sub)
+    fill("Y1")
+    tt("Xm", "Xk:0:64@pm", "H2", mul)
+    scan("PP", "R8:0:64", "Xm", mul)
+    ts("P6", "PP:7:64:8", 1.0 / 6, -2.5 / 6, mul, add)
+    ts("P48", "PP:7:64:8", 48.0, None, mul)
+    cp("Pu", "PP:7:64:8", sem="p_ok")
     ts("T1", "P6", -287.0, None, mul)
     tt("e1", "T1", "P48", add)
     cp("off1", "e1")
+    cp("win1:0:288@off1:0:8", "cval")
     need("x_in")
     v(V.quantize_mx, "qx", [], T.sx[:], T.xs[:], sem="qxr")
-    cp("win1:0:288@off1:0:8", "cval")
     tr("tr1", "win1")
 
     def across(k, lst, nb, sem):
@@ -213,27 +214,22 @@ def rank_program(g, core, T, topo):
     def picks(out, a, b, src, n, lst, c, e, sem):
         inc(A.activation(T[out][:, a:b], T[src][:, 0:n].indirect(T[lst][:, c:e]), AF.Copy), sem)
 
-    pickc("q1", 0, 288, "qx", 256, "l1", 0, 18, "q1c")
+    pickc("land1", 0, OUT, "qx", 256, "l1", 0, 18, "q1c")
 
     need("pf", 1)
     need("kz", 2)
     cp("keywin:0:1536@tou:0:8", "Pf")
-    cp("l1o:0:3", "l1:%d:%d" % (3 * R, 3 * R + 3), sem="l1own")
     tr("trk", "keywin")
-    need("l1own")
-    pickc("land1", 0, 48, "qx", 256, "l1o", 0, 3, "o1c")
     tt("Xs", "trk:0:1536:32", "trk:16:1536:32", add, sem="xsr")
 
     need("gi3", ng["gi3"])
-    need("ac", 11)
+    need("ac", 14)
     nr = arrivals(False)
     need("rc", nr)
     need("cown", 1)
     cp("G", "cnt:0:64@lg:0:6")
-    tt("Nn", "G:48:96", "G:0:48", sub)
+    scan("off", "G:47:95", "G:0:48", add, sub)
     ts("Lf", "G:0:48", 1.0 / 6, "cL", mul, add)
-    scan("Ai", "R8b", "Nn", mul)
-    tt("off", "Ai", "G:48:96", sub)
     ts("FF", "off", 1.0 / 6, R / 6 - 2.5 / 6, mul, add)
     tt("off2:0:6", "off:%d:%d" % (8 * R, 8 * R + 6), "c6:0:6", add)
     tt("D:1:49", "cb", "FF", sub)
@@ -241,12 +237,12 @@ def rank_program(g, core, T, topo):
     tt("DD", "D:1:49", "D:0:48", sub)
     tt("GE", "Bt:0:48@rl:0:9", "Jr", O.is_le)
     tt("M", "DD:0:48@rl:0:9", "GE", mul)
-    scan("Sm", "R8", "M", mul)
+    scan("Sm", "R8L", "M", mul)
     tt("lf", "Sm:5:144:8", "J2r", add)
     ts("l2", "lf", "F4:2:3", float(W1 - 1), add, O.min, sem="l2r")
     ts("l2o:0:3", "lf:%d:%d" % (3 * R, 3 * R + 3), "F4:2:3", float(W1 - 1), add, O.min, sem="l2own")
     need("l2r")
-    need("o1c")
+    need("q1c", 1)
     need("rc1", arrivals(False))
     pickc("q2", 0, 288, "land1", W1, "l2", 0, 18, "q2c")
     need("l2own")
@@ -277,16 +273,16 @@ def rank_program(g, core, T, topo):
     def part(o, h):
         return slice(256 * o + 128 * h, 256 * o + 128 * h + 128), slice(512 * (2 * o + h), 512 * (2 * o + h) + 128)
 
-    for h in range(2):
-        y, p = part(0, h)
-        need("mm0%d" % h, 1)
-        inc(V.tensor_copy(T.ys[:, y], T.ps[:, p]), "y0")
+    for o, h in ((0, 0), (1, 0), (0, 1)):
+        y, p = part(o, h)
+        need("mm%d%d" % (o, h), 1)
+        inc(V.tensor_copy(T.ys[:, y], T.ps[:, p]), "y%d%d" % (o, h))
 
     w(E, "qwr", 1)
     for h in range(2):
         w(E, "q3c%d" % h, 1)
         w(E, "q3s%d" % h, 1)
-        for o in range(2):
+        for o in ((0, 1), (1, 0))[h]:
             inc(E.matmul_mx(T.ps[:, part(o, h)[1]], T.qw[:, 128 * o:128 * o + 128], T.sw[:, 128 * o:128 * o + 128],
                             T.q3[:, 128 * h:128 * h + 128], T.s3[:, 128 * h:128 * h + 128], True, True), "mm%d%d" % (o, h))
 
@@ -298,7 +294,10 @@ def rank_program(g, core, T, topo):
         act("cb:%d:48:8" % r, "zer:0:6", "ac", bias=float(base1(r, R) - r) if r < N else 0.0)
     act("Y2", "zer:0:32", "ac")
     act("D:0:1", "zer:0:1", "ac")
-    act("cnt:48:64", "zer:0:16", "ac")
+    act("cnt:56:64", "zer:0:8", "ac")
+    w(A, "r8", 1)
+    for c in (0, 48, 96):
+        act("R8L:%d:%d" % (c, c + 48), "R8:0:48", "ac")
     w(A, "x_in", tot["x_in"])
     act("keywin:0:1024", "xs", "kz", scale=0.0)
     act("keywin:1024:1536", "xs:0:512", "kz", scale=0.0)
@@ -309,13 +308,11 @@ def rank_program(g, core, T, topo):
     act("Pf", "idt:0:256@Pu:0:8", "pf")
     w(A, "qxr", 1)
     w(A, "l1r", 2)
-    picks("s1", 0, 288, "sx", 256, "l1", 0, 18, "q1s")
-    w(A, "l1own", 1)
-    picks("lans1", 0, 48, "sx", 256, "l1o", 0, 3, "o1s")
+    picks("lans1", 0, OUT, "sx", 256, "l1", 0, 18, "q1s")
     w(A, "xsr", 1)
     act("Xin:%d:%d" % (8 * R, 8 * R + 8), "Xs:%d:%d" % (8 * R, 8 * R + 8), "xown")
     w(A, "l2r", 1)
-    w(A, "o1s", 1)
+    w(A, "q1s", 1)
     w(A, "rs1", arrivals(True))
     picks("s2", 0, 288, "lans1", W1, "l2", 0, 18, "q2s")
     w(A, "l2own", 1)
@@ -325,21 +322,20 @@ def rank_program(g, core, T, topo):
     w(A, "rs2", arrivals(True))
     for h in range(2):
         picks("s3", 128 * h, 128 * h + 128, "lans2", 288, "l3", 8 * h, 8 * h + 8, "q3s%d" % h)
-    for h in range(2):
-        y, p = part(1, h)
-        w(A, "mm1%d" % h, 1)
-        inc(A.activation(T.ys[:, y], T.ps[:, p], AF.Copy), "y1")
-    for q, o in ((S, 0), (A, 1)):
-        w(q, "y%d" % o, 2)
-        inc(q.dma_start(T.y[:, 256 * o:256 * o + 256], T.ys[:, 256 * o:256 * o + 256]), "st", 16)
+    y, p = part(1, 1)
+    w(A, "mm11", 1)
+    inc(A.activation(T.ys[:, y], T.ps[:, p], AF.Copy), "y11")
+    for q, o, h in ((S, 0, 0), (S, 1, 0), (S, 0, 1), (A, 1, 1)):
+        w(q, "y%d%d" % (o, h), 1)
+        inc(q.dma_start(T.y[:, part(o, h)[0]], T.ys[:, part(o, h)[0]]), "st", 16)
 
     w(g, "sb", 1)
     fused(lambda d: T.Sb[:, 0:8], lambda d: T.cnt[:, 8 * R:8 * R + 8], "rc", False)
     w(g, "q1c", 1)
-    fused(lambda d: T.q1[:, 48 * d:48 * d + C1].bitcast(dt.uint8),
+    fused(lambda d: T.land1[:, 48 * d:48 * d + C1].bitcast(dt.uint8),
           lambda d: T.land1[:, base1(R, d):base1(R, d) + C1].bitcast(dt.uint8), "rc1", False)
     w(g, "q1s", 1)
-    fused(lambda d: T.s1[:, 48 * d:48 * d + C1], lambda d: T.lans1[:, base1(R, d):base1(R, d) + C1], "rs1", True)
+    fused(lambda d: T.lans1[:, 48 * d:48 * d + C1], lambda d: T.lans1[:, base1(R, d):base1(R, d) + C1], "rs1", True)
     w(g, "xsr", 1)
     fused(lambda d: T.Xs[:, 8 * d:8 * d + 8], lambda d: T.Xin[:, 8 * R:8 * R + 8], "rx", False)
     w(g, "q2c", 1)

@@ -7,13 +7,14 @@ OUT = 6 * 48
 W1 = OUT + 5 * C1
 _C = "float8_e4m3fn_x4"
 _BUFS = {
-    "int32": "toh 8 p8 4 Dc 48 Dc2 64 I4 4 tt3 9 dest 8 P6 8 Lf 48 FF 48 P6x 48 u6 48",
-    "uint16": "repa 4 repd 4 pm 4 dup 4 lg 6 rl 10 tou 8 Pu 8 off1 8 l1 18 l2 18 l2o 4 l3 16",
-    "bfloat16": "xs 1024 ws 1024 cval 128 idt 256 Sb 8 win1 288 tr1 288 Pf 128 keywin 1536 trk 1536 Xs 48 Xin 48 cnt 64",
-    "float32": "R8 64 R8L 144 cvr 128 Jr 144 J2r 18 c6 8 F4 4 hf 1 cL 1 c1 1 kk 6 kk4 4 kkm 9 dupb 4 cb 48 zer 32 LE 48 "
-               "H2 64 Cb 264 Cd 48 B3 96 QQ 64 Z 64 K 8 Xk 64 Xm 64 PP 64 P48 8 T1 8 e1 8 Y1 32 Yt1 32 Yd1 64 Z1 64 G 96 "
-               "off 48 Bt 48 D 50 DD 48 off2 8 GE 144 M 144 Sm 144 lf 18 tx 48 mk 48 V1 48 V2 48 V3 48 "
-               "V4 48 Wx 48 b1 24 b2 8 Y2 32 Yt2 32 Yd2 64 Z2 64 ys 512",
+    "int32": "toh 8 p8 8 Dc 48 Dc2 64 I4 6 dest 8 P6 8 tt3 9 FF 48 u6 8",
+    "uint16": "repa 4 repd 4 pm 4 repo 4 lc 2 lc2 2 rl 10 tou 8 Pu 8 off1 8 l1 32 l2 18 l2o 4 l3 16",
+    "bfloat16": "xs 1024 ws 1024 cval 128 idt 288 SbT 32 Sb 32 win1 320 TR 608 Pf 128 keywin 1536 trk 1536 Xs 48 Xin 48 "
+                "cnt 64",
+    "float32": "R8 64 R8L 144 R16 128 Rc 128 cvr 128 Jr 144 J2r 18 F4 6 hf 1 c1 1 c8 1 q6 1 eh 1 eg 1 eh2 1 pv 1 kk4 4 "
+               "kkm 9 k8 2 cb 48 zer 32 LE 48 H2 64 Cb 264 Cd 64 B3 96 QQ 64 Z 32 X2 128 PP 128 Pq 8 Ps 8 x6 8 w1 8 e1 8 "
+               "Y1 19 G 64 off 64 bf 48 XO 64 PO 64 uu 8 cs 8 D 50 DD 48 GE 144 M 144 Sm 144 lf 18 b1 24 b2 8 Y3 64 YY 64 "
+               "ys 512",
     _C: "qx 256 qw 256 land1 512 q2 288 land2 288 q3 256",
     "uint8": "sx 256 sw 256 lans1 512 s2 288 lans2 288 s3 256",
 }
@@ -22,7 +23,7 @@ for _d, _s in _BUFS.items():
     _p = _s.split()
     for _n, _w in zip(_p[0::2], _p[1::2]):
         SCRATCH[_n] = ("sbuf", [128, int(_w)], _d)
-SEMAPHORES = ("v gi1 gi2 gi3 to_in x_in w_in zr r8 ac sb p_ok pf kz l1r qxr q1c q1s xsr xown cown l2r "
+SEMAPHORES = ("v gi0 gi1 gi2 gi3 gi4 to_in x_in w_in zr r8 ac ac2 hfr sb p_ok pf kz l1r qxr q1c q1s xsr xown cown l2r "
               "l2own q2c q2s o2c o2s l3r qwr q3c0 q3c1 q3s0 q3s1 mm00 mm01 mm10 mm11 y00 y01 y10 y11 st "
               "rc rx rc1 rs1 rc2 rs2 ls").split()
 
@@ -57,8 +58,8 @@ def rank_program(g, core, T, topo):
     def need(sem, n=None):
         n = tot[sem] if n is None else n
         if waited.get(sem, 0) < n:
-            waited[sem] = max(n, tot.get(sem, 0)) if sem == "v" else n
-            V.wait_ge(T.sem[sem], waited[sem])
+            waited[sem] = n
+            V.wait_ge(T.sem[sem], n)
 
     def w(q, sem, n):
         q.wait_ge(T.sem[sem], n)
@@ -69,8 +70,14 @@ def rank_program(g, core, T, topo):
         a = T[f[0]][:, slice(*[int(i) for i in f[1:]])] if f[1:] else T[f[0]][:]
         return a.indirect(ap(off)) if off else a
 
+    made = {"p8": ("gi0", 1), "Dc2": ("gi1", 3), "kk4": ("gi1", 3), "k8": ("gi1", 3), "Dc": ("gi2", 1),
+            "kkm": ("gi3", 3), "R16": ("ac2", 2), "cval": ("ac2", 2), "cnt": ("gi4", 4), "Jr": ("gi4", 4),
+            "J2r": ("gi4", 4)}
+
     def reads(s):
         for n in s.replace("@", ":").split(":"):
+            if n in made:
+                need(*made[n])
             if n in last:
                 need(*last[n])
 
@@ -95,8 +102,8 @@ def rank_program(g, core, T, topo):
     def scan(out, i, j, op0, op1=O.add, **k):
         v(V.tensor_tensor_scan, out, [i, j], 0.0, op0, op1, **k)
 
-    def tr(out, i):
-        v(V.transpose, out, [i])
+    def tr(out, i, **k):
+        v(V.transpose, out, [i], **k)
 
     def fill(s, c=0.0, **k):
         v(V.memset, s, [], c, **k)
@@ -128,84 +135,75 @@ def rank_program(g, core, T, topo):
         inc(g.iota(ap(n), pat, base, ch, **k), sem)
 
     fl = {"allow_small_or_imprecise_dtypes": True}
-    iota("p8", [[0, 4]], "gi1", 0, 1)
-    iota("kk4", [[2, 4]], "gi1", **fl)
+    iota("p8", [[0, 8]], "gi0", 0, 1)
     iota("Dc2", [[0, 8], [1, 8]], "gi1")
-    iota("dupb", [[16, 2], [0, 2]], "gi1", **fl)
+    iota("kk4", [[2, 4]], "gi1", **fl)
+    iota("k8", [[8, 2]], "gi1", **fl)
     iota("Dc", [[256, 6], [0, 8]], "gi2", 256)
-    iota("cvr", [[16, 8], [1, 8], [128, 2]], "gi2", **fl)
-    iota("kk", [[1, 2], [2, 3]], "gi2", **fl)
-    iota("kkm", [[2, 9]], "gi2", -1, **fl)
-    iota("idt", [[1, 256]], "gi3", 1, **fl)
-    iota("c6", [[6, 8]], "gi3", -288, **fl)
-    iota("J2r", [[0, 6], [16, 3]], "gi3", **fl)
-    iota("Jr", [[0, 6], [16, 3], [-1, 8]], "gi3", **fl)
-    iota("cnt:48:56", [[-256, 8]], "gi3", **fl)
-    ng = dict(tot)
+    iota("Rc", [[0, 8], [1, 16]], "gi3", **fl)
+    iota("cvr", [[16, 8], [1, 8], [128, 2]], "gi3", **fl)
+    iota("kkm", [[2, 9]], "gi3", -1, **fl)
 
     fill("zer", sem="zr")
-    fill("Sb")
-    fill("win1")
-    fill("B3")
-    fill("Cb")
-    need("gi1", ng["gi1"])
+    fill("B3:0:32")
     ts("I4:0:1", "p8:0:1", 7, None, band)
     ts("I4:1:2", "p8:1:2", 3, 1, shr, band)
     ts("I4:2:3", "p8:2:3", 15, None, band)
     ts("I4:3:4", "p8:3:4", 4, 1, shr, band)
+    ts("I4:4:5", "p8:4:5", 1, None, band)
+    ts("I4:5:6", "p8:5:6", 1, 7, shr, band)
     ts("R8", "Dc2", 1.0, None, O.min, sem="r8")
     cp("F4", "I4")
-    fill("Xk:48:64")
-    ts("repa:0:3", "zer:0:3", "F4:0:1", None, add)
+    fill("Cb")
+    ts("hf", "F4:3:4", 8.0, None, mul, sem="hfr")
+    ts("repa", "zer:0:4", "F4:0:1", None, add)
     ts("repd", "kk4", "F4:1:2", None, add)
-    ts("dup", "dupb", "F4:2:3", None, add)
-    ts("hf", "F4:3:4", 8.0, None, mul)
     ts("c1", "F4:0:1", 8.0, "F4:1:2", mul, add)
-    ts("cL", "F4:2:3", -1.0, (2.5 - R) / 6, mul, add)
-    need("gi2", ng["gi2"])
-    ts("cval", "cvr", "hf", None, add)
+    ts("eh", "F4:4:5", "F4:3:4", 10.0, O.is_equal, mul)
+    ts("eg", "F4:4:5", "F4:3:4", "F4:5:6", O.is_gt, add)
     ts("pm", "kk4", "c1", None, add)
-    ts("tt3", "kkm", "F4:1:2", 1.0 / 3, add, mul)
-    ts("lg", "kk", "c1", None, add)
+    tt("pv", "eh", "eg", add)
+    fill("win1")
+    ts("lc", "k8", "pv", 18.0, add, O.min)
 
     need("to_in")
     tt("LE", "toh:0:8@repa:0:3", "Dc", O.is_lt)
     ts("dest", "toh", 8, None, shr)
     scan("Cb:8:56", "R8:0:48", "LE", mul)
-    cp("tou", "toh")
-    tr("B3:32:64", "Cb:15:264:8")
     tt("H2", "dest:0:8@repd", "Dc2", O.is_equal)
+    tr("B3:64:96", "Cb:15:264:8")
+    tr("B3:32:64", "Cb:7:256:8")
+    need("ac", 17)
+    tt("Cd:0:48", "Cb:0:48", "Cb:8:56", sub)
     scan("QQ", "B3:32:96", "B3:0:64", add, sub)
-    ts("rl:0:9", "tt3", 8.0, "F4:0:1", mul, add)
-    tr("Z", "QQ")
-    tt("Cd", "Cb:8:56", "Cb:0:48", sub)
-    tt("K:0:6", "Z:0:6", "Z:31:37", add)
-    tt("Sb:1:7", "Z:0:6", "Z:32:38", add, sem="sb")
-    tt("Xk:0:48", "K:0:6@repd:0:3", "Cd", sub)
-    fill("Y1")
-    tt("Xm", "Xk:0:64@pm", "H2", mul)
-    scan("PP", "R8:0:64", "Xm", mul)
-    ts("P6", "PP:7:64:8", 1.0 / 6, -2.5 / 6, mul, add)
-    ts("P48", "PP:7:64:8", 48.0, None, mul)
-    cp("Pu", "PP:7:64:8", sem="p_ok")
-    ts("T1", "P6", -287.0, None, mul)
-    tt("e1", "T1", "P48", add)
-    cp("off1", "e1")
-    cp("win1:0:288@off1:0:8", "cval")
+    tt("X2:1:128:2", "Cd:0:64@pm", "H2", mul)
+    tr("Z", "QQ:32:64")
+    ts("SbT", "zer", "QQ:63:64", None, add)
+    tt("X2:0:128:2", "Z:0:8@repa", "H2", mul)
+    tr("Sb", "SbT", sem="sb")
+    scan("PP", "R16", "X2", mul)
+    cp("tou", "toh")
+    ts("P6", "PP:15:128:16", 1.0 / 6, -2.5 / 6, mul, add)
+    ts("Pq", "PP:15:128:16", 48.0 / 287, None, mul)
+    ts("Ps", "PP:15:128:16", 1.0 / 6, None, mul)
+    tt("e1", "P6", "Pq", sub)
+    tt("x6", "P6", "Ps", sub)
+    ts("off1", "e1", -287.0, 16.0, mul, add)
+    ts("tt3", "kkm", "F4:1:2", 1.0 / 3, add, mul)
+    ts("q6", "F4:2:3", -6.0, None, mul)
+    cp("win1:0:320@off1:0:8", "cval")
     need("x_in")
     v(V.quantize_mx, "qx", [], T.sx[:], T.xs[:], sem="qxr")
-    tr("tr1", "win1")
-
-    def across(k, lst, nb, sem):
-        tr("Yt" + k, "Y" + k)
-        cp("Yd" + k, "Yt%s:0:32@dup:0:4" % k)
-        tr("Z" + k, "Yd" + k)
-        cp("%s:0:%d:2" % (lst, 2 * nb), "Z%s:0:%d" % (k, nb), sem=sem)
-        cp("%s:1:%d:2" % (lst, 2 * nb), "Z%s:32:%d" % (k, 32 + nb), sem=sem)
-        need(sem)
-
-    tt("Y1:0:9", "tr1:0:288:32", "tr1:16:288:32", add)
-    across("1", "l1", 9, "l1r")
+    tr("TR:0:320", "win1")
+    tr("TR:320:608", "win1:16:304")
+    ts("rl:0:9", "tt3", 8.0, "F4:0:1", mul, add)
+    ts("c8", "F4:0:1", 8.0, float(R), mul, add)
+    tt("Y1", "TR:0:608:32", "TR:16:608:32", add)
+    ts("repo", "zer:0:4", "c8", None, add)
+    ts("w1", "x6", -288.0, float(R), mul, add)
+    cp("l1", "Y1@lc", sem="l1r")
+    ts("eh2", "F4:4:5", "F4:3:4", 32.0, O.not_equal, mul)
+    need("l1r")
     need("qxr")
 
     def pickc(out, a, b, src, n, lst, c, e, sem):
@@ -216,35 +214,38 @@ def rank_program(g, core, T, topo):
 
     pickc("land1", 0, OUT, "qx", 256, "l1", 0, 18, "q1c")
 
-    need("pf", 1)
-    need("kz", 2)
-    cp("keywin:0:1536@tou:0:8", "Pf")
-    tr("trk", "keywin")
-    tt("Xs", "trk:0:1536:32", "trk:16:1536:32", add, sem="xsr")
-
-    need("gi3", ng["gi3"])
-    need("ac", 14)
     nr = arrivals(False)
     need("rc", nr)
     need("cown", 1)
-    cp("G", "cnt:0:64@lg:0:6")
-    scan("off", "G:47:95", "G:0:48", add, sub)
-    ts("Lf", "G:0:48", 1.0 / 6, "cL", mul, add)
-    ts("FF", "off", 1.0 / 6, R / 6 - 2.5 / 6, mul, add)
-    tt("off2:0:6", "off:%d:%d" % (8 * R, 8 * R + 6), "c6:0:6", add)
+    cp("G:16:64", "cnt:0:64@pm:0:3")
+    scan("off:0:48", "G:15:63", "G:8:56", add, sub)
+    reads("q6")
+    v(V.tensor_tensor_scan, "bf", ["G:15:63", "G:7:55"], ap("q6"), add, sub)
+    tt("XO", "off:0:64@repo", "H2", mul)
+    ts("FF", "off:0:48", 1.0 / 6, R / 6 - 2.5 / 6, mul, add)
+    scan("PO", "R8:0:64", "XO", mul)
     tt("D:1:49", "cb", "FF", sub)
-    tt("Bt", "Lf", "FF", add)
+    tt("uu", "PO:7:64:8", "PP:15:128:16", add)
+    tt("GE", "bf:0:48@rl:0:9", "Jr", O.is_lt)
+    ts("u6", "uu", 1.0 / 6, -2.5 / 6, mul, add)
     tt("DD", "D:1:49", "D:0:48", sub)
-    tt("GE", "Bt:0:48@rl:0:9", "Jr", O.is_le)
+    tt("cs", "u6", "w1", add)
+    ts("lc2", "zer:0:2", "eh2", "F4:5:6", add, add)
+    cp("Pu", "cs", sem="p_ok")
     tt("M", "DD:0:48@rl:0:9", "GE", mul)
     scan("Sm", "R8L", "M", mul)
+    need("kz", 2)
+    need("pf", 1)
+    cp("keywin:0:1536@tou:0:8", "Pf")
     tt("lf", "Sm:5:144:8", "J2r", add)
+    tr("trk", "keywin")
     ts("l2", "lf", "F4:2:3", float(W1 - 1), add, O.min, sem="l2r")
-    ts("l2o:0:3", "lf:%d:%d" % (3 * R, 3 * R + 3), "F4:2:3", float(W1 - 1), add, O.min, sem="l2own")
+    tt("Xs", "trk:0:1536:32", "trk:16:1536:32", add, sem="xsr")
     need("l2r")
     need("q1c", 1)
     need("rc1", arrivals(False))
     pickc("q2", 0, 288, "land1", W1, "l2", 0, 18, "q2c")
+    ts("l2o:0:3", "lf:%d:%d" % (3 * R, 3 * R + 3), "F4:2:3", float(W1 - 1), add, O.min, sem="l2own")
     need("l2own")
     pickc("land2", 48 * R, 48 * R + 48, "land1", W1, "l2o", 0, 3, "o2c")
     need("w_in")
@@ -252,19 +253,14 @@ def rank_program(g, core, T, topo):
 
     need("rx", nr)
     need("xown", 1)
-    ts("P6x", "Xin", 1.0 / 6, -3.5 / 6, mul, add)
-    tt("tx", "off2:0:6@repd:0:3", "Xin", add)
-    ts("mk", "Xin", 0.0, None, O.is_gt)
-    ts("Wx", "Xin", 48.0, None, mul)
-    ts("V1", "P6x", -288.0, None, mul)
-    ts("u6", "tx", 1.0 / 6, -3.5 / 6, mul, add)
-    tt("V2", "V1", "Wx", add)
-    tt("V3", "V2", "u6", add)
-    tt("V4", "V3", "mk", mul)
-    tt("b1", "V4:0:24", "V4:24:48", add)
+    tt("b1", "Xin:0:24", "Xin:24:48", add)
     tt("b2", "b1:0:8", "b1:8:16", add)
-    tt("Y2:0:8", "b2", "b1:16:24", add)
-    across("2", "l3", 8, "l3r")
+    tt("Y3:24:32", "b2", "b1:16:24", add)
+    tr("YY:0:32", "Y3:0:32")
+    tr("YY:32:64", "Y3:0:32")
+    tr("Y3:32:64", "YY:16:48")
+    ts("l3", "Y3:24:64@lc2:0:1", 144.0, None, add, sem="l3r")
+    need("l3r")
     need("o2c")
     need("rc2", arrivals(False))
     for h in range(2):
@@ -290,25 +286,32 @@ def rank_program(g, core, T, topo):
         inc(A.activation(ap(out), ap(i), f, **k), sem)
 
     w(A, "zr", 1)
-    for r in range(8):
-        act("cb:%d:48:8" % r, "zer:0:6", "ac", bias=float(base1(r, R) - r) if r < N else 0.0)
-    act("Y2", "zer:0:32", "ac")
+    act("Cd:48:64", "zer:0:16", "ac")
+    act("off:48:64", "zer:0:16", "ac")
+    act("G:0:16", "zer:0:16", "ac")
+    act("Y3:0:32", "zer:0:32", "ac")
     act("D:0:1", "zer:0:1", "ac")
     act("cnt:56:64", "zer:0:8", "ac")
+    for r in range(8):
+        act("cb:%d:48:8" % r, "zer:0:6", "ac", bias=float(base1(r, R) - r) if r < N else 0.0)
     w(A, "r8", 1)
     for c in (0, 48, 96):
         act("R8L:%d:%d" % (c, c + 48), "R8:0:48", "ac")
+    w(A, "gi3", 3)
+    act("R16", "Rc", "ac2", AF.Sign)
+    w(A, "hfr", 1)
+    act("cval", "cvr", "ac2", AF.Identity, bias=ap("hf"))
     w(A, "x_in", tot["x_in"])
     act("keywin:0:1024", "xs", "kz", scale=0.0)
     act("keywin:1024:1536", "xs:0:512", "kz", scale=0.0)
     w(A, "sb", 1)
-    act("cnt:%d:%d" % (8 * R, 8 * R + 8), "Sb", "cown")
-    w(A, "gi3", ng["gi3"])
-    w(A, "p_ok", 1)
-    act("Pf", "idt:0:256@Pu:0:8", "pf")
+    act("cnt:%d:%d" % (8 * R, 8 * R + 8), "Sb:0:8", "cown")
     w(A, "qxr", 1)
-    w(A, "l1r", 2)
+    w(A, "l1r", 1)
     picks("lans1", 0, OUT, "sx", 256, "l1", 0, 18, "q1s")
+    w(A, "gi4", 4)
+    w(A, "p_ok", 1)
+    act("Pf", "idt:0:288@Pu:0:8", "pf")
     w(A, "xsr", 1)
     act("Xin:%d:%d" % (8 * R, 8 * R + 8), "Xs:%d:%d" % (8 * R, 8 * R + 8), "xown")
     w(A, "l2r", 1)
@@ -317,7 +320,7 @@ def rank_program(g, core, T, topo):
     picks("s2", 0, 288, "lans1", W1, "l2", 0, 18, "q2s")
     w(A, "l2own", 1)
     picks("lans2", 48 * R, 48 * R + 48, "lans1", W1, "l2o", 0, 3, "o2s")
-    w(A, "l3r", 2)
+    w(A, "l3r", 1)
     w(A, "o2s", 1)
     w(A, "rs2", arrivals(True))
     for h in range(2):
@@ -331,6 +334,10 @@ def rank_program(g, core, T, topo):
 
     w(g, "sb", 1)
     fused(lambda d: T.Sb[:, 0:8], lambda d: T.cnt[:, 8 * R:8 * R + 8], "rc", False)
+    iota("cnt:48:56", [[-256, 8]], "gi4", -256, **fl)
+    iota("Jr", [[0, 6], [96, 3], [-6, 8]], "gi4", 6, **fl)
+    iota("J2r", [[0, 6], [16, 3]], "gi4", **fl)
+    iota("idt", [[1, 288]], "gi4", -144, **fl)
     w(g, "q1c", 1)
     fused(lambda d: T.land1[:, 48 * d:48 * d + C1].bitcast(dt.uint8),
           lambda d: T.land1[:, base1(R, d):base1(R, d) + C1].bitcast(dt.uint8), "rc1", False)

@@ -7,14 +7,14 @@ OUT = 6 * 48
 W1 = OUT + 5 * C1
 _C = "float8_e4m3fn_x4"
 _BUFS = {
-    "int32": "toh 8 p8 8 Dc 48 Dc2 64 I4 6 dest 8 P6 8 tt3 9 FF 48 u6 8",
-    "uint16": "repa 4 repd 4 pm 4 repo 4 lc 2 lc2 2 rl 10 tou 8 Pu 8 off1 8 l1 32 l2 18 l2o 4 l3 16",
-    "bfloat16": "xs 1024 ws 1024 cval 128 idt 288 SbT 32 Sb 32 win1 320 TR 608 Pf 128 keywin 1536 trk 1536 Xs 48 Xin 48 "
+    "int32": "toh 8 p8 8 Dc 48 Dc2 64 I4 6 dest 8 P6 8 FF 56 Q6 8 U6 8",
+    "uint16": "repa 4 repd 4 pm 4 lc 2 lc2 2 tou 8 Pu 8 off1 8 l1 32 l2 18 l2o 4 l3 16",
+    "bfloat16": "xs 1024 ws 1024 cval 128 idt 256 SbT 32 Sb 32 win1 320 TR 608 Pf 128 keywin 1536 trk 1536 Xs 48 Xin 48 "
                 "cnt 64",
-    "float32": "R8 64 R8L 144 R16 128 Rc 128 cvr 128 Jr 144 J2r 18 F4 6 hf 1 c1 1 c8 1 q6 1 eh 1 eg 1 eh2 1 pv 1 kk4 4 "
-               "kkm 9 k8 2 cb 48 zer 32 LE 48 H2 64 Cb 264 Cd 64 B3 96 QQ 64 Z 32 X2 128 PP 128 Pq 8 Ps 8 x6 8 w1 8 e1 8 "
-               "Y1 19 G 64 off 64 bf 48 XO 64 PO 64 uu 8 cs 8 D 50 DD 48 GE 144 M 144 Sm 144 lf 18 b1 24 b2 8 Y3 64 YY 64 "
-               "ys 512",
+    "float32": "R8 64 R16 128 Rc 128 cvr 128 F4 6 hf 1 c1 1 q6 1 eh 1 eg 1 eh2 1 pv 1 cq 3 kk4 4 k8 2 kd 7 KP 56 LR 48 "
+               "zer 32 LE 48 H2 64 Cb 264 Cd 64 B3 96 QQ 64 Z 32 X2 128 PP 128 Pq 8 e1 8 Y1 19 G 64 off 56 bf 48 OR 48 "
+               "DN 48 NG0 48 NG1 48 NG2 48 S0 48 S1 48 S2 48 B 48 b1 24 b2 8 b3 8 x1 24 x2 8 x3 8 xq 8 xw 8 uu 8 ee 8 "
+               "g2 8 Y3 64 YY 64 ys 512",
     _C: "qx 256 qw 256 land1 512 q2 288 land2 288 q3 256",
     "uint8": "sx 256 sw 256 lans1 512 s2 288 lans2 288 s3 256",
 }
@@ -23,9 +23,8 @@ for _d, _s in _BUFS.items():
     _p = _s.split()
     for _n, _w in zip(_p[0::2], _p[1::2]):
         SCRATCH[_n] = ("sbuf", [128, int(_w)], _d)
-SEMAPHORES = ("v gi0 gi1 gi2 gi3 gi4 to_in x_in w_in zr r8 ac ac2 hfr sb p_ok pf kz l1r qxr q1c q1s xsr xown cown l2r "
-              "l2own q2c q2s o2c o2s l3r qwr q3c0 q3c1 q3s0 q3s1 mm00 mm01 mm10 mm11 y00 y01 y10 y11 st "
-              "rc rx rc1 rs1 rc2 rs2 ls").split()
+SEMAPHORES = ("v gi to_in x_in w_in zr f4r ac sb p_ok pf kz l1r qxr q1c q1s xsr xown cown l2r l2own q2c q2s "
+              "o2c o2s l3r qwr q3c0 q3c1 q3s0 q3s1 mm00 mm01 mm10 mm11 y00 y01 y10 y11 st rc rx rc1 rs1 rc2 rs2 ls").split()
 
 
 def _shares(src, cores, topo, flip):
@@ -50,6 +49,7 @@ def rank_program(g, core, T, topo):
     shr, band = O.arith_shift_right, O.bitwise_and
     AF = ActivationFunctionType
     tot, last, waited = {}, {}, {}
+    made = {}
 
     def inc(inst, sem, n=1):
         inst.then_inc(T.sem[sem], n)
@@ -69,10 +69,6 @@ def rank_program(g, core, T, topo):
         f = s.split(":")
         a = T[f[0]][:, slice(*[int(i) for i in f[1:]])] if f[1:] else T[f[0]][:]
         return a.indirect(ap(off)) if off else a
-
-    made = {"p8": ("gi0", 1), "Dc2": ("gi1", 3), "kk4": ("gi1", 3), "k8": ("gi1", 3), "Dc": ("gi2", 1),
-            "kkm": ("gi3", 3), "R16": ("ac2", 2), "cval": ("ac2", 2), "cnt": ("gi4", 4), "Jr": ("gi4", 4),
-            "J2r": ("gi4", 4)}
 
     def reads(s):
         for n in s.replace("@", ":").split(":"):
@@ -125,86 +121,117 @@ def rank_program(g, core, T, topo):
             tot["ls"] = tot.get("ls", 0) + len(sh[c])
         g.remote_dma_fused(t, local_sem=T.sem.ls)
 
+    def common(c):
+        o = [k for k in cores if k != c]
+        return [e for e in topo.engines(c, o[0]) if all(e in topo.engines(c, k) for k in o)]
+
     for b in range(4):
         inc((S, A)[b % 2].dma_start(T.toh[32 * b:32 * b + 32, :], T.to[:, :]), "to_in", 16)
     inc(S.dma_start(T.xs[:, 0:512], T.x[:, 0:512]), "x_in", 16)
     inc(A.dma_start(T.xs[:, 512:1024], T.x[:, 512:1024]), "x_in", 16)
     inc(S.dma_start(T.ws[:], T.w[:]), "w_in", 16)
 
-    def iota(n, pat, sem, base=0, ch=0, **k):
-        inc(g.iota(ap(n), pat, base, ch, **k), sem)
+    def iota(n, pat, base=0, ch=0, **k):
+        inc(g.iota(ap(n), pat, base, ch, **k), "gi")
+        made[n] = ("gi", tot["gi"])
 
     fl = {"allow_small_or_imprecise_dtypes": True}
-    iota("p8", [[0, 8]], "gi0", 0, 1)
-    iota("Dc2", [[0, 8], [1, 8]], "gi1")
-    iota("kk4", [[2, 4]], "gi1", **fl)
-    iota("k8", [[8, 2]], "gi1", **fl)
-    iota("Dc", [[256, 6], [0, 8]], "gi2", 256)
-    iota("Rc", [[0, 8], [1, 16]], "gi3", **fl)
-    iota("cvr", [[16, 8], [1, 8], [128, 2]], "gi3", **fl)
-    iota("kkm", [[2, 9]], "gi3", -1, **fl)
+    iota("p8", [[0, 8]], 0, 1)
+    iota("kk4", [[2, 4]], **fl)
+    iota("Dc", [[256, 6], [0, 8]], 256)
+    iota("kd", [[1, 7]], **fl)
+    iota("Dc2", [[0, 8], [1, 8]])
+    iota("Rc", [[0, 8], [1, 16]], **fl)
+    iota("cvr", [[16, 8], [1, 8], [128, 2]], **fl)
+    iota("k8", [[8, 2]], **fl)
+
+    def act(out, i, sem, f=AF.Copy, **k):
+        inc(A.activation(ap(out), ap(i), f, **k), sem)
+
+    def const(out, i, f=AF.Copy, **k):
+        act(out, i, "ac", f, **k)
+        made[out.split(":")[0]] = ("ac", tot["ac"])
+
+    w(A, "zr", 1)
+    for b, n in (("Cb:63:264:8", 26), ("Cb:0:8", 8), ("B3:0:32", 32), ("Cd:48:64", 16), ("G:0:8", 8), ("off:0:8", 8),
+                 ("Y3:0:32", 32), ("cnt:48:64", 16)):
+        const(b, "zer:0:%d" % n)
+    lam = [6.0 * base1(r, R) for r in range(N)] + [292.0 + R, 0.0]
+    w(A, "gi", made["kd"][1])
+    for r in range(8):
+        const("KP:%d:56:8" % r, "kd", bias=lam[r], scale=6.0 if r < 7 else -298.0)
+    for r in range(N):
+        const("LR:%d:%d" % (8 * r, 8 * r + 8), "zer:0:8", bias=lam[r] + 6.0 * R + 258)
+    w(A, "ac", made["KP"][1])
+    const("G:8:16", "KP:0:8")
+    w(A, "gi", made["Rc"][1])
+    const("R16", "Rc", AF.Sign)
+    for c in (0, 128, 256):
+        const("win1:%d:%d" % (c, min(c + 128, 320)), "Rc:0:%d" % min(128, 320 - c), scale=0.0)
+    w(A, "f4r", 1)
+    const("hf", "F4:3:4", scale=8.0)
+    const("q6", "F4:2:3", scale=-6.0)
+    for a in range(3):
+        const("cq:%d:%d" % (a, a + 1), "F4:2:3", bias=16.0 * a)
+    w(A, "ac", made["hf"][1])
+    w(A, "gi", made["cvr"][1])
+    const("cval", "cvr", AF.Identity, bias=ap("hf"))
+    w(A, "x_in", tot["x_in"])
+    act("keywin:0:1024", "xs", "kz", scale=0.0)
+    act("keywin:1024:1536", "xs:0:512", "kz", scale=0.0)
 
     fill("zer", sem="zr")
-    fill("B3:0:32")
     ts("I4:0:1", "p8:0:1", 7, None, band)
     ts("I4:1:2", "p8:1:2", 3, 1, shr, band)
     ts("I4:2:3", "p8:2:3", 15, None, band)
     ts("I4:3:4", "p8:3:4", 4, 1, shr, band)
     ts("I4:4:5", "p8:4:5", 1, None, band)
     ts("I4:5:6", "p8:5:6", 1, 7, shr, band)
-    ts("R8", "Dc2", 1.0, None, O.min, sem="r8")
-    cp("F4", "I4")
-    fill("Cb")
-    ts("hf", "F4:3:4", 8.0, None, mul, sem="hfr")
+    cp("F4", "I4", sem="f4r")
     ts("repa", "zer:0:4", "F4:0:1", None, add)
     ts("repd", "kk4", "F4:1:2", None, add)
     ts("c1", "F4:0:1", 8.0, "F4:1:2", mul, add)
-    ts("eh", "F4:4:5", "F4:3:4", 10.0, O.is_equal, mul)
-    ts("eg", "F4:4:5", "F4:3:4", "F4:5:6", O.is_gt, add)
+    ts("R8", "Dc2", 1.0, None, O.min)
     ts("pm", "kk4", "c1", None, add)
-    tt("pv", "eh", "eg", add)
-    fill("win1")
-    ts("lc", "k8", "pv", 18.0, add, O.min)
 
     need("to_in")
     tt("LE", "toh:0:8@repa:0:3", "Dc", O.is_lt)
     ts("dest", "toh", 8, None, shr)
+    need(*made["Cb"])
     scan("Cb:8:56", "R8:0:48", "LE", mul)
     tt("H2", "dest:0:8@repd", "Dc2", O.is_equal)
     tr("B3:64:96", "Cb:15:264:8")
     tr("B3:32:64", "Cb:7:256:8")
-    need("ac", 17)
+    need(*made["Cd"])
     tt("Cd:0:48", "Cb:0:48", "Cb:8:56", sub)
+    ts("eh", "F4:4:5", "F4:3:4", 10.0, O.is_equal, mul)
     scan("QQ", "B3:32:96", "B3:0:64", add, sub)
     tt("X2:1:128:2", "Cd:0:64@pm", "H2", mul)
-    tr("Z", "QQ:32:64")
     ts("SbT", "zer", "QQ:63:64", None, add)
-    tt("X2:0:128:2", "Z:0:8@repa", "H2", mul)
+    tr("Z", "QQ:32:64")
     tr("Sb", "SbT", sem="sb")
+    tt("X2:0:128:2", "Z:0:8@repa", "H2", mul)
+    ts("eg", "F4:4:5", "F4:3:4", "F4:5:6", O.is_gt, add)
     scan("PP", "R16", "X2", mul)
     cp("tou", "toh")
     ts("P6", "PP:15:128:16", 1.0 / 6, -2.5 / 6, mul, add)
     ts("Pq", "PP:15:128:16", 48.0 / 287, None, mul)
-    ts("Ps", "PP:15:128:16", 1.0 / 6, None, mul)
+    cp("Pu", "PP:15:128:16", sem="p_ok")
     tt("e1", "P6", "Pq", sub)
-    tt("x6", "P6", "Ps", sub)
+    tt("pv", "eh", "eg", add)
     ts("off1", "e1", -287.0, 16.0, mul, add)
-    ts("tt3", "kkm", "F4:1:2", 1.0 / 3, add, mul)
-    ts("q6", "F4:2:3", -6.0, None, mul)
+    ts("lc", "k8", "pv", 18.0, add, O.min)
     cp("win1:0:320@off1:0:8", "cval")
     need("x_in")
     v(V.quantize_mx, "qx", [], T.sx[:], T.xs[:], sem="qxr")
     tr("TR:0:320", "win1")
     tr("TR:320:608", "win1:16:304")
-    ts("rl:0:9", "tt3", 8.0, "F4:0:1", mul, add)
-    ts("c8", "F4:0:1", 8.0, float(R), mul, add)
-    tt("Y1", "TR:0:608:32", "TR:16:608:32", add)
-    ts("repo", "zer:0:4", "c8", None, add)
-    ts("w1", "x6", -288.0, float(R), mul, add)
-    cp("l1", "Y1@lc", sem="l1r")
     ts("eh2", "F4:4:5", "F4:3:4", 32.0, O.not_equal, mul)
-    need("l1r")
+    tt("Y1", "TR:0:608:32", "TR:16:608:32", add)
+    ts("lc2", "zer:0:2", "eh2", "F4:5:6", add, add)
+    cp("l1", "Y1@lc", sem="l1r")
     need("qxr")
+    need("l1r")
 
     def pickc(out, a, b, src, n, lst, c, e, sem):
         inc(V.tensor_copy(T[out][:, a:b].bitcast(dt.uint32), T[src][:, 0:n].bitcast(dt.uint32).indirect(T[lst][:, c:e])), sem)
@@ -214,52 +241,60 @@ def rank_program(g, core, T, topo):
 
     pickc("land1", 0, OUT, "qx", 256, "l1", 0, 18, "q1c")
 
-    nr = arrivals(False)
-    need("rc", nr)
-    need("cown", 1)
-    cp("G:16:64", "cnt:0:64@pm:0:3")
-    scan("off:0:48", "G:15:63", "G:8:56", add, sub)
-    reads("q6")
-    v(V.tensor_tensor_scan, "bf", ["G:15:63", "G:7:55"], ap("q6"), add, sub)
-    tt("XO", "off:0:64@repo", "H2", mul)
-    ts("FF", "off:0:48", 1.0 / 6, R / 6 - 2.5 / 6, mul, add)
-    scan("PO", "R8:0:64", "XO", mul)
-    tt("D:1:49", "cb", "FF", sub)
-    tt("uu", "PO:7:64:8", "PP:15:128:16", add)
-    tt("GE", "bf:0:48@rl:0:9", "Jr", O.is_lt)
-    ts("u6", "uu", 1.0 / 6, -2.5 / 6, mul, add)
-    tt("DD", "D:1:49", "D:0:48", sub)
-    tt("cs", "u6", "w1", add)
-    ts("lc2", "zer:0:2", "eh2", "F4:5:6", add, add)
-    cp("Pu", "cs", sem="p_ok")
-    tt("M", "DD:0:48@rl:0:9", "GE", mul)
-    scan("Sm", "R8L", "M", mul)
-    need("kz", 2)
+    need("kz")
     need("pf", 1)
     cp("keywin:0:1536@tou:0:8", "Pf")
-    tt("lf", "Sm:5:144:8", "J2r", add)
     tr("trk", "keywin")
-    ts("l2", "lf", "F4:2:3", float(W1 - 1), add, O.min, sem="l2r")
     tt("Xs", "trk:0:1536:32", "trk:16:1536:32", add, sem="xsr")
+
+    need("rc", sum(len(common(c)) for c in cores if c != core))
+    need("cown", 1)
+    need(*made["G"])
+    tt("G:16:64", "cnt:0:64@pm:0:3", "KP:8:56", add)
+    scan("off:8:56", "G:15:63", "G:8:56", add, sub)
+    reads("q6")
+    v(V.tensor_tensor_scan, "bf", ["G:15:63", "G:7:55"], ap("q6"), add, sub)
+    ts("FF:0:49", "off:7:56", 1.0 / 6, R / 6 - 2.5 / 6, mul, add)
+    for a in range(3):
+        ts("NG%d" % a, "bf", 96.0 * a + 6, None, O.is_ge)
+    tt("DN", "FF:1:49", "FF:0:48", sub)
+    tt("OR", "off:%d:%d@repd:0:3" % (8 * R + 8, 8 * R + 16), "LR", add)
+    for a in range(3):
+        scan("S%d" % a, "DN", "NG%d" % a, add, mul)
+    for a in range(3):
+        ts("l2:%d:18:3" % a, "S%d:6:48:8" % a, "cq:%d:%d" % (a, a + 1), float(W1 - 1), add, O.min, sem="l2r")
+    cp("l2o:0:3", "l2:%d:%d" % (3 * R, 3 * R + 3), sem="l2own")
     need("l2r")
     need("q1c", 1)
     need("rc1", arrivals(False))
     pickc("q2", 0, 288, "land1", W1, "l2", 0, 18, "q2c")
-    ts("l2o:0:3", "lf:%d:%d" % (3 * R, 3 * R + 3), "F4:2:3", float(W1 - 1), add, O.min, sem="l2own")
     need("l2own")
     pickc("land2", 48 * R, 48 * R + 48, "land1", W1, "l2o", 0, 3, "o2c")
     need("w_in")
     v(V.quantize_mx, "qw", [], T.sw[:], T.ws[:], sem="qwr")
 
-    need("rx", nr)
+    need("rx", arrivals(False))
     need("xown", 1)
-    tt("b1", "Xin:0:24", "Xin:24:48", add)
+    tt("B", "OR", "Xin", O.min)
+    tt("x1", "Xin:0:24", "Xin:24:48", add)
+    tt("b1", "B:0:24", "B:24:48", add)
+    tt("x2", "x1:0:8", "x1:8:16", add)
     tt("b2", "b1:0:8", "b1:8:16", add)
-    tt("Y3:24:32", "b2", "b1:16:24", add)
+    tt("x3", "x2", "x1:16:24", add)
+    tt("b3", "b2", "b1:16:24", add)
+    ts("xq", "x3", 1.0 / 1024, None, mul)
+    ts("Q6", "x3", 1.0 / 6144, -3.5 / 6, mul, add)
+    tt("uu", "b3", "xq", add)
+    ts("ee", "Q6", -288.0, -91.0, mul, add)
+    ts("U6", "uu", 1.0 / 6, -3.5 / 6, mul, add)
+    ts("xw", "x3", 48.0 / 1024, None, mul)
+    tt("g2", "U6", "ee", add)
+    need(*made["Y3"])
+    tt("Y3:24:32", "g2", "xw", add)
     tr("YY:0:32", "Y3:0:32")
     tr("YY:32:64", "Y3:0:32")
     tr("Y3:32:64", "YY:16:48")
-    ts("l3", "Y3:24:64@lc2:0:1", 144.0, None, add, sem="l3r")
+    cp("l3", "Y3:24:64@lc2:0:1", sem="l3r")
     need("l3r")
     need("o2c")
     need("rc2", arrivals(False))
@@ -282,39 +317,17 @@ def rank_program(g, core, T, topo):
             inc(E.matmul_mx(T.ps[:, part(o, h)[1]], T.qw[:, 128 * o:128 * o + 128], T.sw[:, 128 * o:128 * o + 128],
                             T.q3[:, 128 * h:128 * h + 128], T.s3[:, 128 * h:128 * h + 128], True, True), "mm%d%d" % (o, h))
 
-    def act(out, i, sem, f=AF.Copy, **k):
-        inc(A.activation(ap(out), ap(i), f, **k), sem)
-
-    w(A, "zr", 1)
-    act("Cd:48:64", "zer:0:16", "ac")
-    act("off:48:64", "zer:0:16", "ac")
-    act("G:0:16", "zer:0:16", "ac")
-    act("Y3:0:32", "zer:0:32", "ac")
-    act("D:0:1", "zer:0:1", "ac")
-    act("cnt:56:64", "zer:0:8", "ac")
-    for r in range(8):
-        act("cb:%d:48:8" % r, "zer:0:6", "ac", bias=float(base1(r, R) - r) if r < N else 0.0)
-    w(A, "r8", 1)
-    for c in (0, 48, 96):
-        act("R8L:%d:%d" % (c, c + 48), "R8:0:48", "ac")
-    w(A, "gi3", 3)
-    act("R16", "Rc", "ac2", AF.Sign)
-    w(A, "hfr", 1)
-    act("cval", "cvr", "ac2", AF.Identity, bias=ap("hf"))
-    w(A, "x_in", tot["x_in"])
-    act("keywin:0:1024", "xs", "kz", scale=0.0)
-    act("keywin:1024:1536", "xs:0:512", "kz", scale=0.0)
     w(A, "sb", 1)
     act("cnt:%d:%d" % (8 * R, 8 * R + 8), "Sb:0:8", "cown")
+    w(A, "p_ok", 1)
+    w(A, "gi", tot["gi"] + 1)
+    act("Pf", "idt:0:256@Pu:0:8", "pf")
     w(A, "qxr", 1)
     w(A, "l1r", 1)
     picks("lans1", 0, OUT, "sx", 256, "l1", 0, 18, "q1s")
-    w(A, "gi4", 4)
-    w(A, "p_ok", 1)
-    act("Pf", "idt:0:288@Pu:0:8", "pf")
     w(A, "xsr", 1)
     act("Xin:%d:%d" % (8 * R, 8 * R + 8), "Xs:%d:%d" % (8 * R, 8 * R + 8), "xown")
-    w(A, "l2r", 1)
+    w(A, "l2r", 3)
     w(A, "q1s", 1)
     w(A, "rs1", arrivals(True))
     picks("s2", 0, 288, "lans1", W1, "l2", 0, 18, "q2s")
@@ -333,11 +346,12 @@ def rank_program(g, core, T, topo):
         inc(q.dma_start(T.y[:, part(o, h)[0]], T.ys[:, part(o, h)[0]]), "st", 16)
 
     w(g, "sb", 1)
-    fused(lambda d: T.Sb[:, 0:8], lambda d: T.cnt[:, 8 * R:8 * R + 8], "rc", False)
-    iota("cnt:48:56", [[-256, 8]], "gi4", -256, **fl)
-    iota("Jr", [[0, 6], [96, 3], [-6, 8]], "gi4", 6, **fl)
-    iota("J2r", [[0, 6], [16, 3]], "gi4", **fl)
-    iota("idt", [[1, 288]], "gi4", -144, **fl)
+    others = [topo.addr(c) for c in cores if c != core]
+    tot["ls"] = len(common(core))
+    g.remote_dma_fused([RemoteDMATransfer(dst_ids=[DstId(rid=a[0], pnc=a[1]) for a in others], remote_sem=T.sem.rc,
+                                          dma_engine_mask=sum(1 << e for e in common(core)), srcs=[T.Sb[:, 0:8]],
+                                          dsts=[T.cnt[:, 8 * R:8 * R + 8] for a in others])], local_sem=T.sem.ls)
+    iota("idt", [[1024, 256]], 1024, **fl)
     w(g, "q1c", 1)
     fused(lambda d: T.land1[:, 48 * d:48 * d + C1].bitcast(dt.uint8),
           lambda d: T.land1[:, base1(R, d):base1(R, d) + C1].bitcast(dt.uint8), "rc1", False)

from concourse.bass import DstId, RemoteDMATransfer
from concourse.mybir import dt, AluOpType, ActivationFunctionType

N = 6
C1, C2 = 43, 48
OUT = 6 * 48
W1 = OUT + 5 * C1
_C = "float8_e4m3fn_x4"
_BUFS = {
    "int32": "toh 8 p8 8 Dc 48 Dc2 64 I4 6 dest 8 P6 8 FF 56 Q6 8 U6 8",
    "uint16": "repa 4 repd 4 pm 4 lc 2 lc2 2 tou 8 Pu 8 off1 8 l1 32 l2 18 l2o 4 l3 16",
    "bfloat16": "xs 1024 ws 1024 cval 128 idt 256 SbT 32 Sb 32 win1 320 TR 608 Pf 128 keywin 1536 trk 1536 Xs 48 Xin 48 "
                "cnt 64",
    "float32": "R8 64 R16 128 Rc 128 cvr 128 F4 6 hf 1 c1 1 q6 1 eh 1 eg 1 eh2 1 pv 1 cq 3 kk4 4 k8 2 kd 7 KP 56 LR 48 "
               "zer 32 LE 48 H2 64 Cb 264 Cd 64 B3 96 QQ 64 Z 32 X2 128 PP 128 Pq 8 e1 8 Y1 19 G 64 off 56 bf 48 OR 48 "
               "DN 48 NG0 48 NG1 48 NG2 48 S0 48 S1 48 S2 48 B 48 b1 24 b2 8 b3 8 x1 24 x2 8 x3 8 xq 8 xw 8 uu 8 ee 8 "
               "g2 8 Y3 64 YY 64 ys 512",
    _C: "qx 256 qw 256 land1 512 q2 288 land2 288 q3 256",
    "uint8": "sx 256 sw 256 lans1 512 s2 288 lans2 288 s3 256",
}
SCRATCH = {"ps": ("psum", [128, 2048], "float32")}
for _d, _s in _BUFS.items():
    _p = _s.split()
    for _n, _w in zip(_p[0::2], _p[1::2]):
        SCRATCH[_n] = ("sbuf", [128, int(_w)], _d)
SEMAPHORES = ("v gi to_in x_in w_in zr f4r ac sb p_ok pf kz l1r qxr q1c q1s xsr xown cown l2r l2own q2c q2s "
              "o2c o2s l3r qwr q3c0 q3c1 q3s0 q3s1 mm00 mm01 mm10 mm11 y00 y01 y10 y11 st rc rx rc1 rs1 rc2 rs2 ls").split()


def _shares(src, cores, topo, flip):
    k = cores.index(src)
    ds = cores[k + 1:] + cores[:k]
    ds = sorted(ds, key=lambda c: topo.die(c) == topo.die(src))
    e = topo.engines(src, ds[0])
    h, w = len(e) // 2, len(e) // 8
    if flip:
        e = e[h:] + e[:h]
    return {c: e[:h] if i == 0 else e[h + (i - 1) * w:h + i * w] for i, c in enumerate(ds)}


def rank_program(g, core, T, topo):
    R = T.rank_of(core)
    if R is None:
        return
    cores = list(T.cores)
    V, A, S, E = g.vector, g.scalar, g.sync, g.tensor
    O = AluOpType
    add, sub, mul = O.add, O.subtract, O.mult
    shr, band = O.arith_shift_right, O.bitwise_and
    AF = ActivationFunctionType
    tot, last, waited = {}, {}, {}
    made = {}

    def inc(inst, sem, n=1):
        inst.then_inc(T.sem[sem], n)
        tot[sem] = tot.get(sem, 0) + n

    def need(sem, n=None):
        n = tot[sem] if n is None else n
        if waited.get(sem, 0) < n:
            waited[sem] = n
            V.wait_ge(T.sem[sem], n)

    def w(q, sem, n):
        q.wait_ge(T.sem[sem], n)

    def ap(s):
        s, _, off = s.partition("@")
        f = s.split(":")
        a = T[f[0]][:, slice(*[int(i) for i in f[1:]])] if f[1:] else T[f[0]][:]
        return a.indirect(ap(off)) if off else a

    def reads(s):
        for n in s.replace("@", ":").split(":"):
            if n in made:
                need(*made[n])
            if n in last:
                need(*last[n])

    def v(call, out, ins, *more, sem="v"):
        for s in ins + ([out] if "@" in out else []):
            reads(s)
        inc(call(ap(out), *[ap(s) for s in ins], *more), sem)
        last[out.split(":")[0].split("@")[0]] = (sem, tot[sem])

    def ts(out, i, s1, s2, *ops, **k):
        for s in (s1, s2):
            if isinstance(s, str):
                reads(s)
        v(V.tensor_scalar, out, [i], *[ap(s) if isinstance(s, str) else s for s in (s1, s2)], *ops, **k)

    def tt(out, i, j, op, **k):
        v(V.tensor_tensor, out, [i, j], op, **k)

    def cp(out, i, **k):
        v(V.tensor_copy, out, [i], **k)

    def scan(out, i, j, op0, op1=O.add, **k):
        v(V.tensor_tensor_scan, out, [i, j], 0.0, op0, op1, **k)

    def tr(out, i, **k):
        v(V.transpose, out, [i], **k)

    def fill(s, c=0.0, **k):
        v(V.memset, s, [], c, **k)

    def base1(r, m):
        return 48 * m if r == m else OUT + C1 * [k for k in range(N) if k != m].index(r)

    def arrivals(flip):
        return sum(len(_shares(c, cores, topo, flip)[core]) for c in cores if c != core)

    def fused(src_of, dst_of, sem, flip):
        sh = _shares(core, cores, topo, flip)
        t = []
        for c in sh:
            rid, pid, _ = topo.addr(c)
            d = cores.index(c)
            t.append(RemoteDMATransfer(dst_ids=[DstId(rid=rid, pnc=pid)], dma_engine_mask=sum(1 << e for e in sh[c]),
                                       remote_sem=T.sem[sem], src=src_of(d), dst=dst_of(d)))
            tot["ls"] = tot.get("ls", 0) + len(sh[c])
        g.remote_dma_fused(t, local_sem=T.sem.ls)

    def common(c):
        o = [k for k in cores if k != c]
        return [e for e in topo.engines(c, o[0]) if all(e in topo.engines(c, k) for k in o)]

    for b in range(4):
        inc((S, A)[b % 2].dma_start(T.toh[32 * b:32 * b + 32, :], T.to[:, :]), "to_in", 16)
    inc(S.dma_start(T.xs[:, 0:512], T.x[:, 0:512]), "x_in", 16)
    inc(A.dma_start(T.xs[:, 512:1024], T.x[:, 512:1024]), "x_in", 16)
    inc(S.dma_start(T.ws[:], T.w[:]), "w_in", 16)

    def iota(n, pat, base=0, ch=0, **k):
        inc(g.iota(ap(n), pat, base, ch, **k), "gi")
        made[n] = ("gi", tot["gi"])

    fl = {"allow_small_or_imprecise_dtypes": True}
    iota("p8", [[0, 8]], 0, 1)
    iota("kk4", [[2, 4]], **fl)
    iota("Dc", [[256, 6], [0, 8]], 256)
    iota("kd", [[1, 7]], **fl)
    iota("Dc2", [[0, 8], [1, 8]])
    iota("Rc", [[0, 8], [1, 16]], **fl)
    iota("cvr", [[16, 8], [1, 8], [128, 2]], **fl)
    iota("k8", [[8, 2]], **fl)

    def act(out, i, sem, f=AF.Copy, **k):
        inc(A.activation(ap(out), ap(i), f, **k), sem)

    def const(out, i, f=AF.Copy, **k):
        act(out, i, "ac", f, **k)
        made[out.split(":")[0]] = ("ac", tot["ac"])

    w(A, "zr", 1)
    for b, n in (("Cb:63:264:8", 26), ("Cb:0:8", 8), ("B3:0:32", 32), ("Cd:48:64", 16), ("G:0:8", 8), ("off:0:8", 8),
                 ("Y3:0:32", 32), ("cnt:48:64", 16)):
        const(b, "zer:0:%d" % n)
    lam = [6.0 * base1(r, R) for r in range(N)] + [292.0 + R, 0.0]
    w(A, "gi", made["kd"][1])
    for r in range(8):
        const("KP:%d:56:8" % r, "kd", bias=lam[r], scale=6.0 if r < 7 else -298.0)
    for r in range(N):
        const("LR:%d:%d" % (8 * r, 8 * r + 8), "zer:0:8", bias=lam[r] + 6.0 * R + 258)
    w(A, "ac", made["KP"][1])
    const("G:8:16", "KP:0:8")
    w(A, "gi", made["Rc"][1])
    const("R16", "Rc", AF.Sign)
    for c in (0, 128, 256):
        const("win1:%d:%d" % (c, min(c + 128, 320)), "Rc:0:%d" % min(128, 320 - c), scale=0.0)
    w(A, "f4r", 1)
    const("hf", "F4:3:4", scale=8.0)
    const("q6", "F4:2:3", scale=-6.0)
    for a in range(3):
        const("cq:%d:%d" % (a, a + 1), "F4:2:3", bias=16.0 * a)
    w(A, "ac", made["hf"][1])
    w(A, "gi", made["cvr"][1])
    const("cval", "cvr", AF.Identity, bias=ap("hf"))
    w(A, "x_in", tot["x_in"])
    act("keywin:0:1024", "xs", "kz", scale=0.0)
    act("keywin:1024:1536", "xs:0:512", "kz", scale=0.0)

    fill("zer", sem="zr")
    ts("I4:0:1", "p8:0:1", 7, None, band)
    ts("I4:1:2", "p8:1:2", 3, 1, shr, band)
    ts("I4:2:3", "p8:2:3", 15, None, band)
    ts("I4:3:4", "p8:3:4", 4, 1, shr, band)
    ts("I4:4:5", "p8:4:5", 1, None, band)
    ts("I4:5:6", "p8:5:6", 1, 7, shr, band)
    cp("F4", "I4", sem="f4r")
    ts("repa", "zer:0:4", "F4:0:1", None, add)
    ts("repd", "kk4", "F4:1:2", None, add)
    ts("c1", "F4:0:1", 8.0, "F4:1:2", mul, add)
    ts("R8", "Dc2", 1.0, None, O.min)
    ts("pm", "kk4", "c1", None, add)

    need("to_in")
    tt("LE", "toh:0:8@repa:0:3", "Dc", O.is_lt)
    ts("dest", "toh", 8, None, shr)
    need(*made["Cb"])
    scan("Cb:8:56", "R8:0:48", "LE", mul)
    tt("H2", "dest:0:8@repd", "Dc2", O.is_equal)
    tr("B3:64:96", "Cb:15:264:8")
    tr("B3:32:64", "Cb:7:256:8")
    need(*made["Cd"])
    tt("Cd:0:48", "Cb:0:48", "Cb:8:56", sub)
    ts("eh", "F4:4:5", "F4:3:4", 10.0, O.is_equal, mul)
    scan("QQ", "B3:32:96", "B3:0:64", add, sub)
    tt("X2:1:128:2", "Cd:0:64@pm", "H2", mul)
    ts("SbT", "zer", "QQ:63:64", None, add)
    tr("Z", "QQ:32:64")
    tr("Sb", "SbT", sem="sb")
    tt("X2:0:128:2", "Z:0:8@repa", "H2", mul)
    ts("eg", "F4:4:5", "F4:3:4", "F4:5:6", O.is_gt, add)
    scan("PP", "R16", "X2", mul)
    cp("tou", "toh")
    ts("P6", "PP:15:128:16", 1.0 / 6, -2.5 / 6, mul, add)
    ts("Pq", "PP:15:128:16", 48.0 / 287, None, mul)
    cp("Pu", "PP:15:128:16", sem="p_ok")
    tt("e1", "P6", "Pq", sub)
    tt("pv", "eh", "eg", add)
    ts("off1", "e1", -287.0, 16.0, mul, add)
    ts("lc", "k8", "pv", 18.0, add, O.min)
    cp("win1:0:320@off1:0:8", "cval")
    need("x_in")
    v(V.quantize_mx, "qx", [], T.sx[:], T.xs[:], sem="qxr")
    tr("TR:0:320", "win1")
    tr("TR:320:608", "win1:16:304")
    ts("eh2", "F4:4:5", "F4:3:4", 32.0, O.not_equal, mul)
    tt("Y1", "TR:0:608:32", "TR:16:608:32", add)
    ts("lc2", "zer:0:2", "eh2", "F4:5:6", add, add)
    cp("l1", "Y1@lc", sem="l1r")
    need("qxr")
    need("l1r")

    def pickc(out, a, b, src, n, lst, c, e, sem):
        inc(V.tensor_copy(T[out][:, a:b].bitcast(dt.uint32), T[src][:, 0:n].bitcast(dt.uint32).indirect(T[lst][:, c:e])), sem)

    def picks(out, a, b, src, n, lst, c, e, sem):
        inc(A.activation(T[out][:, a:b], T[src][:, 0:n].indirect(T[lst][:, c:e]), AF.Copy), sem)

    pickc("land1", 0, OUT, "qx", 256, "l1", 0, 18, "q1c")

    need("kz")
    need("pf", 1)
    cp("keywin:0:1536@tou:0:8", "Pf")
    tr("trk", "keywin")
    tt("Xs", "trk:0:1536:32", "trk:16:1536:32", add, sem="xsr")

    need("rc", sum(len(common(c)) for c in cores if c != core))
    need("cown", 1)
    need(*made["G"])
    tt("G:16:64", "cnt:0:64@pm:0:3", "KP:8:56", add)
    scan("off:8:56", "G:15:63", "G:8:56", add, sub)
    reads("q6")
    v(V.tensor_tensor_scan, "bf", ["G:15:63", "G:7:55"], ap("q6"), add, sub)
    ts("FF:0:49", "off:7:56", 1.0 / 6, R / 6 - 2.5 / 6, mul, add)
    for a in range(3):
        ts("NG%d" % a, "bf", 96.0 * a + 6, None, O.is_ge)
    tt("DN", "FF:1:49", "FF:0:48", sub)
    tt("OR", "off:%d:%d@repd:0:3" % (8 * R + 8, 8 * R + 16), "LR", add)
    for a in range(3):
        scan("S%d" % a, "DN", "NG%d" % a, add, mul)
    for a in range(3):
        ts("l2:%d:18:3" % a, "S%d:6:48:8" % a, "cq:%d:%d" % (a, a + 1), float(W1 - 1), add, O.min, sem="l2r")
    cp("l2o:0:3", "l2:%d:%d" % (3 * R, 3 * R + 3), sem="l2own")
    need("l2r")
    need("q1c", 1)
    need("rc1", arrivals(False))
    pickc("q2", 0, 288, "land1", W1, "l2", 0, 18, "q2c")
    need("l2own")
    pickc("land2", 48 * R, 48 * R + 48, "land1", W1, "l2o", 0, 3, "o2c")
    need("w_in")
    v(V.quantize_mx, "qw", [], T.sw[:], T.ws[:], sem="qwr")

    need("rx", arrivals(False))
    need("xown", 1)
    tt("B", "OR", "Xin", O.min)
    tt("x1", "Xin:0:24", "Xin:24:48", add)
    tt("b1", "B:0:24", "B:24:48", add)
    tt("x2", "x1:0:8", "x1:8:16", add)
    tt("b2", "b1:0:8", "b1:8:16", add)
    tt("x3", "x2", "x1:16:24", add)
    tt("b3", "b2", "b1:16:24", add)
    ts("xq", "x3", 1.0 / 1024, None, mul)
    ts("Q6", "x3", 1.0 / 6144, -3.5 / 6, mul, add)
    tt("uu", "b3", "xq", add)
    ts("ee", "Q6", -288.0, -91.0, mul, add)
    ts("U6", "uu", 1.0 / 6, -3.5 / 6, mul, add)
    ts("xw", "x3", 48.0 / 1024, None, mul)
    tt("g2", "U6", "ee", add)
    need(*made["Y3"])
    tt("Y3:24:32", "g2", "xw", add)
    tr("YY:0:32", "Y3:0:32")
    tr("YY:32:64", "Y3:0:32")
    tr("Y3:32:64", "YY:16:48")
    cp("l3", "Y3:24:64@lc2:0:1", sem="l3r")
    need("l3r")
    need("o2c")
    need("rc2", arrivals(False))
    for h in range(2):
        pickc("q3", 128 * h, 128 * h + 128, "land2", 288, "l3", 8 * h, 8 * h + 8, "q3c%d" % h)

    def part(o, h):
        return slice(256 * o + 128 * h, 256 * o + 128 * h + 128), slice(512 * (2 * o + h), 512 * (2 * o + h) + 128)

    for o, h in ((0, 0), (1, 0), (0, 1)):
        y, p = part(o, h)
        need("mm%d%d" % (o, h), 1)
        inc(V.tensor_copy(T.ys[:, y], T.ps[:, p]), "y%d%d" % (o, h))

    w(E, "qwr", 1)
    for h in range(2):
        w(E, "q3c%d" % h, 1)
        w(E, "q3s%d" % h, 1)
        for o in ((0, 1), (1, 0))[h]:
            inc(E.matmul_mx(T.ps[:, part(o, h)[1]], T.qw[:, 128 * o:128 * o + 128], T.sw[:, 128 * o:128 * o + 128],
                            T.q3[:, 128 * h:128 * h + 128], T.s3[:, 128 * h:128 * h + 128], True, True), "mm%d%d" % (o, h))

    w(A, "sb", 1)
    act("cnt:%d:%d" % (8 * R, 8 * R + 8), "Sb:0:8", "cown")
    w(A, "p_ok", 1)
    w(A, "gi", tot["gi"] + 1)
    act("Pf", "idt:0:256@Pu:0:8", "pf")
    w(A, "qxr", 1)
    w(A, "l1r", 1)
    picks("lans1", 0, OUT, "sx", 256, "l1", 0, 18, "q1s")
    w(A, "xsr", 1)
    act("Xin:%d:%d" % (8 * R, 8 * R + 8), "Xs:%d:%d" % (8 * R, 8 * R + 8), "xown")
    w(A, "l2r", 3)
    w(A, "q1s", 1)
    w(A, "rs1", arrivals(True))
    picks("s2", 0, 288, "lans1", W1, "l2", 0, 18, "q2s")
    w(A, "l2own", 1)
    picks("lans2", 48 * R, 48 * R + 48, "lans1", W1, "l2o", 0, 3, "o2s")
    w(A, "l3r", 1)
    w(A, "o2s", 1)
    w(A, "rs2", arrivals(True))
    for h in range(2):
        picks("s3", 128 * h, 128 * h + 128, "lans2", 288, "l3", 8 * h, 8 * h + 8, "q3s%d" % h)
    y, p = part(1, 1)
    w(A, "mm11", 1)
    inc(A.activation(T.ys[:, y], T.ps[:, p], AF.Copy), "y11")
    for q, o, h in ((S, 0, 0), (S, 1, 0), (S, 0, 1), (A, 1, 1)):
        w(q, "y%d%d" % (o, h), 1)
        inc(q.dma_start(T.y[:, part(o, h)[0]], T.ys[:, part(o, h)[0]]), "st", 16)

    w(g, "sb", 1)
    others = [topo.addr(c) for c in cores if c != core]
    tot["ls"] = len(common(core))
    g.remote_dma_fused([RemoteDMATransfer(dst_ids=[DstId(rid=a[0], pnc=a[1]) for a in others], remote_sem=T.sem.rc,
                                          dma_engine_mask=sum(1 << e for e in common(core)), srcs=[T.Sb[:, 0:8]],
                                          dsts=[T.cnt[:, 8 * R:8 * R + 8] for a in others])], local_sem=T.sem.ls)
    iota("idt", [[1024, 256]], 1024, **fl)
    w(g, "q1c", 1)
    fused(lambda d: T.land1[:, 48 * d:48 * d + C1].bitcast(dt.uint8),
          lambda d: T.land1[:, base1(R, d):base1(R, d) + C1].bitcast(dt.uint8), "rc1", False)
    w(g, "q1s", 1)
    fused(lambda d: T.lans1[:, 48 * d:48 * d + C1], lambda d: T.lans1[:, base1(R, d):base1(R, d) + C1], "rs1", True)
    w(g, "xsr", 1)
    fused(lambda d: T.Xs[:, 8 * d:8 * d + 8], lambda d: T.Xin[:, 8 * R:8 * R + 8], "rx", False)
    w(g, "q2c", 1)
    fused(lambda d: T.q2[:, 48 * d:48 * d + C2].bitcast(dt.uint8),
          lambda d: T.land2[:, 48 * R:48 * R + C2].bitcast(dt.uint8), "rc2", False)
    w(g, "q2s", 1)
    fused(lambda d: T.s2[:, 48 * d:48 * d + C2], lambda d: T.lans2[:, 48 * R:48 * R + C2], "rs2", True)
    for s in ("v", "ls", "st"):
        w(g, s, tot[s])
